import numpy as np, ml_dtypes
CORES = [36,164,52,180,100,228,116,244]
N = 8
import mx_ref
BF = ml_dtypes.bfloat16
def gentries(a):
    return np.ascontiguousarray(a.reshape(8, 16, -1).transpose(0, 2, 1)).reshape(8, -1)
def gtable(e):
    e = np.asarray(e); return np.ascontiguousarray(e.reshape(8, -1, 16).transpose(0, 2, 1)).reshape(128, -1).astype(np.int32)
def gcols(t, e):
    v = np.concatenate([t.reshape(8, 16, -1, 4), np.zeros((8, 16, 1, 4), BF)], axis=2)
    return np.ascontiguousarray(np.stack([v[g][:, e[g]] for g in range(8)])).reshape(128, -1)
def tile(rs):
    return np.stack(rs, axis=2).reshape(128, -1).astype(BF)
def pick(q, e):
    c = np.concatenate([q[0].reshape(128, -1, 4), np.zeros((128, 1, 4), np.uint8)], axis=1); s = np.concatenate([q[1], np.ones((16, 1), np.uint8)], axis=1)
    return (np.ascontiguousarray(c[:, e].reshape(128, -1)), np.ascontiguousarray(s[:, e]))
def join(*qs):
    return (np.concatenate([q[0] for q in qs], axis=1), np.concatenate([q[1] for q in qs], axis=1))
def put(q, e, v):
    c, s = q[0].reshape(128, -1, 4).copy(), q[1].copy(); c[:, e] = v[0].reshape(128, -1, 4); s[:, e] = v[1]
    return (c.reshape(128, -1), s)
def pk(c, s):
    return (np.ascontiguousarray(c), mx_ref.live(s))
def emit(q):
    return q[0], q[1]
def packed(v, rng):
    q = [mx_ref.quantize(np.ascontiguousarray(v[r])) for r in range(N)]
    return np.stack([a for a, b in q]), np.stack([mx_ref.plane(b, rng) for a, b in q])
def values_of_codes():
    e, c = np.zeros((128, 128, 4), np.float32), np.zeros((128, 2, 4), np.uint8)
    e[np.arange(128), np.arange(128), 0] = 1
    c[:127, :, 0] = np.arange(256).reshape(2, 128).T[:127]
    return mx_ref.matmul(mx_ref.quantize(e.reshape(128, 512).astype(BF)), (c.reshape(128, 8), np.full((16, 2), 127, np.uint8))).T.reshape(-1).astype(np.float64)
CODE_VALUE, SCALE_VALUE = values_of_codes(), 2.0 ** (np.arange(256) - 127.0)
def decode(q):
    return (CODE_VALUE[q[0]].reshape(16, 8, -1, 4) * SCALE_VALUE[q[1]][:, None, :, None] + 0.0).reshape(128, -1).astype(np.float32)
def f(rng, *shape):
    return mx_ref.flush((rng.standard_normal(shape, dtype=np.float32) * np.exp2(rng.integers(-2, 3, shape[:-1] + (1,)))).astype(BF))
def wide(rng, *shape, cols=0):
    v = rng.standard_normal(shape, dtype=np.float32) * np.exp2(rng.integers(-12, 13, shape)).astype(np.float32)
    if cols: v *= np.repeat(np.exp2(rng.integers(-cols, cols + 1, shape[:-2] + (1, shape[-1] // 4))) * (rng.random(shape[:-2] + (1, shape[-1] // 4)) > 0.0625), 4, axis=-1).astype(np.float32)
    return mx_ref.flush(v.astype(BF))
C, M = 320, 16
STEP = [1, 2, 4]
BASE = np.arange(C) // 32 * 32
def big(v):
    v = v.astype(np.float32)
    v[np.abs(v) < np.float32(2.0 ** -16)] = 0
    return v.astype(BF)
def numbers_of(rng):
    return {"x": big(f(rng, N, 128, 4 * C)), "u": np.array(f(rng, N, 128, 512)), "v": np.array(f(rng, N, 128, 512))}
def functions(e):
    return np.stack([gtable(e[r] + BASE) for r in range(N)])
def layers(rng, still=[]):
    w = big(f(rng, N, 128, 2048)).reshape(N, 8, 16, 4, 8, 16, 4)
    for i in still:
        w[:, :, i] = 0
        w[:, :, :, :, :, i] = 0
    return w
def weights(rng, w):
    c, p = packed(np.ascontiguousarray(w).reshape(N, 128, 2048), rng)
    return {"wc": c, "ws": p}
def setup_inputs(rng):
    return {**numbers_of(rng), "fn": functions(rng.integers(0, 32, (N, 8, C))), **weights(rng, layers(rng))}
def setup_inputs_ties(rng):
    d = numbers_of(rng)
    x = d["x"].reshape(N, 8, 16, C, 4)
    even = np.repeat(rng.permutation(C // 32) % 2 == 0, 32)
    k = np.where(even, np.repeat(rng.integers(1, 3, (1, 8, C // 32)), 32, axis=2), rng.integers(0, 3, (N, 8, C)))
    e = rng.integers(0, 32, (N, 8, C))
    e = np.where(even, e[:1], e)
    x[:, :, 0] = 0
    x[:, :, 0, :, 0] = k.astype(np.float32).astype(BF)
    u = d["u"].reshape(N, 128, 128, 4)
    u[:, :, ::16] = 0
    o = rng.permutation(N)
    for r in range(N):
        for h in range(0, 128, 16): u[r, h, h, 0] = 0.0 if r == o[0] else -1.0 if r == o[1] else 1.0
    return {"x": x.reshape(N, 128, 4 * C), "u": u.reshape(N, 128, 512), "v": d["v"], "fn": functions(e), **weights(rng, layers(rng, [0]))}
def setup_inputs_near(rng):
    d = numbers_of(rng)
    x = d["x"].astype(np.float32).reshape(N, 8, 16, C, 4)
    x[:, :, 0] = 0
    x[:, :, 8:] = 0
    far = np.repeat(rng.permutation(C // 32) % 2 == 0, 32)
    c = np.repeat(rng.integers(0, 2, (1, 8, C // 32)) * 2.0 - 1.0, 32, axis=2)
    s = rng.integers(0, 16, (N, 8, C))
    x[:, :, 0, :, 0] = np.where(far, 0.0, c)
    x[:, :, 11, :, 0] = np.where(far, 0.0, 2.0 ** -10)
    x[:, :, 8] = np.where(far[:, None], rng.integers(-1, 2, (N, 8, C, 4)) * 2.0 ** -22, ((s[:, :, :, None] >> np.arange(4)) & 1) * np.exp2(np.arange(4) - 23.0))
    u = d["u"].reshape(N, 128, 128, 4)
    u[:, :, ::16] = 0
    o = rng.permutation(N) % 2
    for r in range(N):
        k = 1.0 if o[r] == 0 else 2.0 ** -30
        for h in range(0, 128, 16):
            u[r, h, h, 0] = k
            u[r, h + 8, h] = k
            u[r, h + 11, h, 0] = k
    return {"x": x.reshape(N, 128, 4 * C).astype(BF), "u": u.reshape(N, 128, 512), "v": d["v"], "fn": functions(rng.integers(0, 32, (N, 8, C))), **weights(rng, layers(rng, [0, 8, 9, 10, 11, 12, 13, 14, 15]))}
def setup_inputs_huge(rng):
    d = numbers_of(rng)
    o = rng.permutation(N)
    k = np.repeat(rng.permutation(C // 32) % 3, 32)
    c = np.where(k == 2, rng.choice([-1.0, 1.0], (N, C)), k * 2.0 - 1.0)
    x = 2.0 ** 30 * (0.6 + 0.4 * rng.random((N, 8, 1, C, 1))) * (1.0 - 0.02 * rng.random((N, 8, 16, C, 4))) * c[:, None, None, :, None]
    a = 2.0 ** 29 * (1.0 - 0.1 * rng.random((N, 8, 16, 8, 4)))
    for g in range(8): a[:, g, :, g] *= 2.0
    for r in range(N):
        if o[r] == 0: a[r] = 2.0 ** 30
        if o[r] % 2 == 1: a[r] *= -1.0
    u = d["u"].reshape(N, 128, 128, 4)
    u[:, :, ::16] = a.reshape(N, 128, 8, 4).astype(np.float32).astype(BF)
    w = np.zeros((N, 128, 4, 128, 4), np.float32)
    i = np.arange(128)
    for b in range(4): w[:, i, b, i, b] = -1
    return {"x": x.astype(np.float32).reshape(N, 128, 4 * C).astype(BF), "u": u.reshape(N, 128, 512), "v": d["v"], "fn": functions(rng.integers(0, 32, (N, 8, C))), **weights(rng, w.astype(BF))}
def setup_inputs_paths(rng):
    d = numbers_of(rng)
    x = d["x"].astype(np.float32).reshape(N, 8, 16, C, 4)
    e, top = np.zeros((N, 8, C // 32, 32), np.int64), np.zeros((N, 8, C // 32), np.int64)
    size = [1, M - 1, M, M + 1, 24, 32]
    o = rng.permutation(8)
    for r in range(N):
        for g in range(8):
            for b in range(C // 32):
                k, a = int(o[r] + g + b) % 8, rng.permutation(32)
                top[r, g, b] = a[0]
                e[r, g, b] = a
                if k == 7: top[r, g, b] = rng.integers(32)
                if k < 6:
                    n = size[k]
                    e[r, g, b] = a[rng.integers(0, n, 32)]
                    e[r, g, b, a[:n]] = np.append(a[1:n], a[n - 1])
    s = rng.integers(0, 3, (N, 8, C // 32, 32)) * 0.5
    np.put_along_axis(s, top[:, :, :, None], 1.5, axis=3)
    x[:, :, 0] = 0
    x[:, :, 0, :, 0] = s.reshape(N, 8, C)
    z = np.exp2(rng.integers(-13, -6, (N, 8, 8, 1, 4)) * 1.0) * (1.0 + (2 * rng.integers(0, 64, (N, 8, 8, 1, 4)) + 1) * 2.0 ** -7) * rng.choice([-1.0, 1.0], (N, 8, 8, 1, 4))
    z[:, :, 0, :, 0] = 1.96875
    x[:, :, 8:] = z
    u = d["u"].reshape(N, 128, 128, 4)
    u[:, :, ::16] = 0
    for h in range(0, 128, 16): u[:, h, h, 0] = 1
    return {"x": x.reshape(N, 128, 4 * C).astype(BF), "u": u.reshape(N, 128, 512), "v": d["v"], "fn": functions(e.reshape(N, 8, C)), **weights(rng, layers(rng, [0, 8, 9, 10, 11, 12, 13, 14, 15]))}
def setup_inputs_spread(rng):
    d = setup_inputs(rng)
    d["x"] = big(wide(rng, N, 128, 4 * C, cols=6))
    return d
def check_inputs(d):
    b = []
    for k in ("x", "u", "v"):
        a = np.abs(d[k].astype(np.float32))
        if not (np.isfinite(a).all() and ((a == 0) | (a >= 2.0 ** -30) & (a <= 2.0 ** 30)).all()): b.append("a value of " + k)
    none, least, most = [emit(mx_ref.quantize(np.full((128, 16), k, np.float32).astype(BF)))[1][0, 0] for k in (0.0, 2.0 ** -30, 2.0 ** 30)]
    for r in range(N):
        if (gentries(d["fn"][r]) // 32 * 32 != BASE).any(): b.append("fn: an entry out of its block")
        if ((d["wc"][r] == 0x7F) | (d["wc"][r] == 0xFF)).any(): b.append("wc: a code that is no number")
        s = mx_ref.live(d["ws"][r])
        if ((s != none) & ((s < least) | (s > most))).any(): b.append("ws: a scale out of range")
    return b
def reread(fun, head):
    row = np.arange(len(fun))
    a = fun
    for k in range(5): a = np.take_along_axis(a, a, axis=1)
    cyc = np.zeros(fun.shape, bool)
    np.put_along_axis(cyc, a, True, axis=1)
    many = np.count_nonzero(cyc, axis=1)
    w = np.take_along_axis(fun, np.argsort(~cyc, axis=1, kind="stable"), axis=1)
    up = fun.copy()
    for j in range(31):
        i = row[j + 1 < many]
        up[i, w[i, j]] = w[i, j + 1]
    root = w[row, many - 1]
    path, at, on = np.full(fun.shape, -1), head, np.ones(len(fun), bool)
    for j in range(32):
        path[:, j] = np.where(on, at, -1)
        on = on & (at != root)
        at = up[row, at]
    q = np.sort(np.where(path < 0, 32, path), axis=1)
    for j in range(32):
        i = row[path[:, j] >= 0]
        up[i, q[i, j]] = path[i, j]
    return up, path
def reference(x, u, v, fn, wc, ws):
    qu = [mx_ref.quantize(u[r]) for r in range(N)]
    lay = [pk(wc[r], ws[r]) for r in range(N)]
    now = [x[r] for r in range(N)]
    fun = np.stack([gentries(fn[r]) - BASE for r in range(N)]).astype(np.int64).reshape(-1, 32)
    row = np.arange(len(fun))
    block = row % (C // 32)
    for t in STEP:
        s = np.stack([mx_ref.matmul(qu[r], mx_ref.quantize(now[r]))[::16] + np.float32(0.0) for r in range(N)])
        fun, path = reread(fun, np.argmax(s.reshape(-1, 32), axis=1))
        to = fun.reshape(N, 8, C) + BASE
        give = np.where(path < 0, -1, path + 32 * block[:, None])[:, :M].reshape(N, 8, -1)
        take = np.full(path.shape, -1)
        for j in range(M):
            i = row[path[:, j] >= 0]
            take[i, path[i, j]] = M * block[i] + j
        take = take.reshape(N, 8, C)
        made, sent = [], []
        for r in range(N):
            z = ((now[r].astype(np.float32) + gcols(now[r], to[r]).astype(np.float32)) * np.float32(0.5)).astype(BF)
            q = mx_ref.quantize(z)
            made.append(tile([mx_ref.matmul(pick(lay[r], np.arange(128 * b, 128 * b + 128)), q) * np.float32(0.03125) + z[:, b::4].astype(np.float32) for b in range(4)]))
            sent.append(mx_ref.quantize(gcols(made[r], give[r])))
        for r in range(N):
            came = gcols(decode(sent[r ^ t]).astype(BF), take[r]).astype(np.float32)
            half = ((made[r].astype(np.float32) + came) * np.float32(0.5)).astype(BF)
            now[r] = np.where(np.repeat(np.repeat(take[r] >= 0, 16, axis=0), 4, axis=1), half, made[r])
    y, fo = np.zeros((N, 128, C), np.float32), np.zeros((N, 8, C), np.float32)
    oc, osc = np.zeros((N, 128, 4 * C), np.uint8), np.zeros((N, 16, C), np.uint8)
    for r in range(N):
        q = mx_ref.quantize(now[r])
        y[r] = mx_ref.matmul(mx_ref.quantize(v[r]), q)
        fo[r] = to[r]
        oc[r], osc[r] = emit(q)
    return {"y": y, "fo": fo, "oc": oc, "osc": osc}

@@ -1,0 +1,592 @@
+import numpy as np
+from concourse.mybir import dt, AluOpType as ALU, AxisListType, ActivationFunctionType as ACT
+
+H = 160
+W1 = 176
+END = 168
+STEP = [1, 2, 4]
+BF, F32, I32, U16, CODE, U8 = "bfloat16", "float32", "int32", "uint16", "float8_e4m3fn_x4", "uint8"
+
+SCRATCH = {}
+for _n, _w, _d in [
+        ("fnb", 20, I32), ("ub", 512, BF), ("vb", 512, BF), ("uq", 128, CODE), ("us", 128, U8), ("uq2", 128, CODE), ("us2", 128, U8),
+        ("vq", 128, CODE), ("vs", 128, U8), ("wq", 512, CODE), ("wsc", 512, U8), ("eb", 2048, BF), ("e16", 128, BF), ("eq", 512, CODE), ("es", 512, U8),
+        ("landq", 736, CODE), ("lands", 736, U8), ("pq", 768, CODE), ("psc", 768, U8), ("pt", 8 * 288, BF),
+        ("ci", 64, I32), ("cf", 64, F32), ("nat", W1, BF), ("tm16", H, BF), ("xl", H, BF), ("xb", H, BF), ("rev", H, BF),
+        ("keyb", H, F32), ("cx0", H, F32), ("cx", H, F32), ("cv", H, BF), ("cvb", H, F32), ("wt", H, BF), ("w0", 2 * W1, F32), ("a0", W1, F32),
+        ("keep", H, BF), ("cm0", H, BF), ("cm", H, BF), ("s32", 256, F32), ("cw", 80, F32), ("cu", 32, U16), ("fob", 320, F32), ("yb", 320, F32)]:
+    SCRATCH[_n] = ("sbuf", [128, _w], _d)
+for _h in "01":
+    for _n, _w, _d in [
+            ("x", 640, BF), ("xh", 4 * 336, BF), ("ka", 40, F32), ("kb", 24, F32), ("z", 640, BF), ("xi", 640, BF), ("z32", 640, BF), ("win", 1024, BF), ("p16", 320, BF),
+            ("xq", H, CODE), ("xs", H, U8), ("zq", H, CODE), ("zs", H, U8),
+            ("fr", 10 * W1, BF), ("tb", 12 * H, BF), ("ls", 16 * 12, U16), ("sa", 112, F32), ("sc", 32, F32), ("kg", H, F32), ("ex", 2 * H + 16, F32),
+            ("up", W1, BF), ("pw", W1 + H, F32), ("ur", 6 * W1, BF), ("wr", 8 * W1, F32), ("wi", W1, I32), ("ar", 6 * W1, F32), ("wa", 2 * W1, F32),
+            ("wk", 3 * W1, I32), ("sm", 256, F32), ("si", 32, I32), ("ck", 32, F32), ("mx", H, F32), ("junk", H, BF), ("lr", 96, U16), ("l2", 32, F32)]:
+        SCRATCH[_n + "_" + _h] = ("sbuf", [128, _w], _d)
+SCRATCH["ps"] = ("psum", [128, 4096], F32)
+
+SEMAPHORES = ["v", "s", "p", "g", "sent", "out"] + ["ld%d" % k for k in range(7)] + ["arr%d" % k for k in range(6)]
+
+PAR = {"cy": 1.0, "g": 1.3, "sc": 3.2, "hop": 70.0, "xhop": 110.0, "load": 2300.0, "rem": 3200.0, "act": 65.0}
+TRIES, JUST, TEMP = 6000, 2, 40.0
+
+
+def size(a):
+    return len(range(a[1], a[2], a[3]))
+
+
+def two(*vs):
+    return all(SCRATCH[a[0]][2] in (BF, U16) for a in vs)
+
+
+def V(buf, a=0, b=None, s=1):
+    return (buf, a, SCRATCH[buf][1][1] if b is None else b, s)
+
+
+def C(buf, k):
+    return (buf, k, k + 1, 1)
+
+
+def ap(T, a):
+    if isinstance(a, tuple):
+        return T[a[0]][:, a[1]:a[2]] if a[3] == 1 else T[a[0]][:, a[1]:a[2]:a[3]]
+    return a
+
+
+def views(*xs):
+    return [a for a in xs if isinstance(a, tuple)]
+
+
+def build(par):
+    ops, now = [], [0]
+    cy, ga = par["cy"], par["g"]
+
+    def op(dur, rd, wr, emit, kind="c", **kw):
+        ops.append(dict(hf=now[0], dur=dur, rd=views(*rd), wr=views(*wr), emit=emit, kind=kind, **kw))
+
+    def vc(n):
+        return max(n, 64) * cy
+
+    def ts(out, a, s1, op0, s2=None, op1=None, idx=None):
+        def emit(q, T, e):
+            x = ap(T, a) if idx is None else ap(T, a).indirect(ap(T, idx))
+            if op1 is None:
+                return q.tensor_scalar(ap(T, out), x, ap(T, s1), None, op0)
+            return q.tensor_scalar(ap(T, out), x, ap(T, s1), ap(T, s2), op0, op1)
+        d = vc(size(out) * (0.5 if two(out, a) else 1)) if idx is None else 50 + ga * size(out)
+        op({"v": d}, [a, s1, s2, idx], [out], emit)
+
+    def tt(out, a, b, o, idx=None):
+        def emit(q, T, e):
+            x = ap(T, a) if idx is None else ap(T, a).indirect(ap(T, idx))
+            return q.tensor_tensor(ap(T, out), x, ap(T, b), o)
+        d = vc(size(out) * (1 if a[0] == "ps" else 2)) if idx is None else 50 + ga * size(out)
+        op({"v": d}, [a, b, idx], [out], emit)
+
+    def cp(out, a):
+        op({"v": vc(size(out))}, [a], [out], lambda q, T, e: q.tensor_copy(ap(T, out), ap(T, a)))
+
+    def lin(out, a, scale=1.0, bias=0.0, idx=None, eng="vs"):
+        def emit(q, T, e):
+            x = ap(T, a) if idx is None else ap(T, a).indirect(ap(T, idx))
+            if e == "s":
+                if isinstance(bias, float) and bias == 0.0:
+                    return q.activation(ap(T, out), x, ACT.Copy, scale=scale) if scale != 1.0 else q.activation(ap(T, out), x, ACT.Copy)
+                return q.activation(ap(T, out), x, ACT.Identity, bias=ap(T, bias), scale=scale)
+            if isinstance(bias, float) and bias == 0.0:
+                return q.tensor_scalar(ap(T, out), x, scale, None, ALU.mult) if scale != 1.0 else q.tensor_copy(ap(T, out), x)
+            return q.tensor_scalar(ap(T, out), x, scale, ap(T, bias), ALU.mult, ALU.add)
+        n = size(out)
+        if idx is None:
+            d = {"v": vc(n * (0.5 if two(out, a) else 1)), "s": par["act"] + n * cy}
+        else:
+            d = {"v": 50 + ga * n, "s": 65 + ga * n}
+        op({e: d[e] for e in eng}, [a, bias, idx], [out], emit)
+
+    def dup(out, a):
+        n = size(out)
+
+        def emit(q, T, e):
+            if e == "g":
+                return q.affine_select(ap(T, out), ap(T, a), [[0, n]], ALU.is_equal, 0.0, 0, 0)
+            return q.tensor_copy(ap(T, out), ap(T, a)) if e == "v" else q.activation(ap(T, out), ap(T, a), ACT.Copy)
+        op({"v": vc(n * (0.5 if two(out, a) else 1)), "s": par["act"] + n * cy, "g": 170 + 2 * cy * n}, [a], [out], emit)
+
+    def scan(out, d0, d1, init, op0, op1):
+        op({"v": vc(size(out) * (0.5 if two(out, d0, d1) else 1))}, [d0, d1], [out],
+           lambda q, T, e: q.tensor_tensor_scan(ap(T, out), ap(T, d0), ap(T, d1), init, op0, op1))
+
+    def fill(out, c):
+        d = {"v": vc(size(out) * (0.5 if two(out) else 1))}
+        if SCRATCH[out[0]][2] != U16:
+            d["g"] = 130 + 2 * cy * size(out)
+        op(d, [], [out], lambda q, T, e: q.memset(ap(T, out), c) if e == "v" else q.iota(ap(T, out), [[0, size(out)]], int(c), 0, allow_small_or_imprecise_dtypes=True))
+
+    def iota(out, pat, base, cm=0):
+        def emit(q, T, e):
+            if SCRATCH[out[0]][2] == I32:
+                return q.iota(ap(T, out), pat, base, cm)
+            return q.iota(ap(T, out), pat, base, cm, allow_small_or_imprecise_dtypes=True)
+        op({"g": 130 + 2 * cy * size(out)}, [], [out], emit)
+
+    def select(out, a, pat, base, cm, fillv):
+        op({"g": 170 + 2 * cy * size(out)}, [a], [out], lambda q, T, e: q.affine_select(ap(T, out), ap(T, a), pat, ALU.is_equal, fillv, base, cm))
+
+    def quant(q_, s_, a):
+        op({"v": 12 + 0.22 * size(a)}, [a], [q_, s_], lambda q, T, e: q.quantize_mx(ap(T, q_), ap(T, s_), ap(T, a)))
+
+    def mm(bank, n, lq, lsc, rq, rsc):
+        out = V("ps", 512 * bank, 512 * bank + n)
+        op({"p": (n + 16) * 1.1}, [lq, lsc, rq, rsc], [out], lambda q, T, e: q.matmul_mx(ap(T, out), ap(T, lq), ap(T, lsc), ap(T, rq), ap(T, rsc), True, True))
+
+    def dma(eng, rd, wr, f, sem, lat):
+        op({eng: 60.0}, rd, wr, lambda q, T, e: q.dma_start(*f(T)), kind="dma", sem=sem, lat=lat)
+
+    def wrap(lst, rep, tmp):
+        scan(tmp, rep, V("cv"), -1.0, ALU.max, ALU.add)
+        ts(lst, (tmp[0], tmp[1] + 15, tmp[2], 16), 256.0, ALU.add)
+
+    L = par["load"]
+    dma("y", [], [V("fnb")], lambda T: (T.fnb[:], T.fn[:]), "ld0", L - 300)
+    dma("s", [], [V("ub")], lambda T: (T.ub[:], T.u[:]), "ld1", L)
+    dma("y", [], [V("x_0")], lambda T: (T.x_0[:], T.x[:, 0:640]), "ld2", L + 200)
+    dma("y", [], [V("x_1")], lambda T: (T.x_1[:], T.x[:, 640:1280]), "ld3", L + 600)
+    dma("y", [], [V("wq")], lambda T: (T.wq[:].bitcast(dt.uint8), T.wc[:]), "ld4", L + 1500)
+    dma("y", [], [V("wsc")], lambda T: (T.wsc[:], T.ws[:]), "ld5", L + 1500)
+    dma("y", [], [V("vb")], lambda T: (T.vb[:], T.v[:]), "ld6", L + 2000)
+
+    ri, rf, r16 = C("ci", 1), C("cf", 0), C("cf", 1)
+    iota(C("ci", 0), [[0, 1]], 0, 1)
+    iota(V("nat"), [[1, W1]], 0)
+    iota(V("tm16"), [[0, 10], [512, 16]], 0)
+    ts(ri, C("ci", 0), 15, ALU.bitwise_and)
+    cp(rf, ri)
+    lin(r16, rf, 1.0, 16.0)
+    ts(C("cf", 2), ri, -512.0, ALU.mult, 256.0, ALU.add)
+    ts(C("cf", 3), ri, -16.0, ALU.mult, 240.0, ALU.add)
+    ts(C("cf", 4), C("cf", 3), C("cf", 3), ALU.mult, 256.0, ALU.add)
+    ts(V("cv"), V("tm16"), C("cf", 2), ALU.add)
+    ts(V("cv", 15, H, 16), V("tm16", 0, H, 16), C("cf", 4), ALU.subtract)
+    lin(V("cvb"), V("cv"), 256.0, eng="s")
+    iota(V("xl"), [[0, 5], [1, 32]], 0)
+    iota(V("rev"), [[-1, H]], END)
+    iota(V("cw", 0, 10), [[0, 5], [16, 2]], 0)
+    ts(V("cu", 0, 10), V("cw", 0, 10), rf, ALU.add)
+    nat32 = V("nat", 0, 32)
+    ts(V("s32", 0, 32), nat32, r16, ALU.is_equal)
+    ts(V("s32", 32, 64), nat32, rf, ALU.is_equal)
+    tt(V("s32", 64, 96), V("s32", 0, 32), V("s32", 32, 64), ALU.subtract)
+    tt(V("wt"), V("s32", 64, 96), V("rev"), ALU.mult, idx=V("cu", 0, 10))
+    ts(V("keep"), V("xl"), 1.0, ALU.min)
+    iota(V("keyb"), [[256, H]], 256)
+    iota(V("cx0"), [[1, 5], [0, 32]], H)
+    select(V("cx"), V("cx0"), [[0, 5], [1, 32]], 0, 0, 1.0e6)
+    iota(V("cw", 16, 26), [[16, 10]], 0)
+    iw = V("cw", 32, 42)
+    ts(iw, V("cw", 16, 26), rf, ALU.add)
+    ts(V("s32", 96, 128), nat32, rf, ALU.is_lt, 128.0, ALU.mult)
+    ts(V("s32", 128, 160), nat32, r16, ALU.is_lt, 65536.0, ALU.mult)
+    ts(V("s32", 160, 192), V("s32", 32, 64), 128.0 * W1, ALU.mult, 1.0, ALU.add)
+    ts(V("s32", 192, 224), V("s32", 0, 32), 65536.0 * W1, ALU.mult)
+    tt(V("s32", 96, 160), V("s32", 96, 160), V("s32", 160, 224), ALU.add)
+    tt(V("s32", 224, 256), V("s32", 96, 128), V("s32", 128, 160), ALU.add)
+    lin(V("w0", 0, H), V("s32", 224, 256), idx=V("cu", 0, 10))
+    fill(V("w0", H, W1), 0.0)
+    dup(V("w0", W1, 2 * W1), V("w0", 0, W1))
+    for k in range(4):
+        ts(C("ci", 2 + k), ri, 1 << k, ALU.bitwise_and)
+        ts(C("cf", 8 + k), C("ci", 2 + k), 256.0 + 8192.0 / (1 << k), ALU.mult, -8192.0, ALU.add)
+    lin(V("a0"), V("nat"), bias=C("cf", 8), eng="s")
+    lin(C("cf", 12), rf, 256.0)
+    ts(C("ci", 6), ri, 1, ALU.arith_shift_right)
+    ts(C("cf", 13), ri, 10.0, ALU.is_ge, -8.0, ALU.mult)
+    ts(C("cf", 14), ri, -10.0, ALU.add, 4.0, ALU.min)
+    blk = C("cf", 15)
+    ts(blk, C("ci", 6), C("cf", 13), ALU.add, C("cf", 14), ALU.max)
+    ts(C("cf", 16), ri, 10.0, ALU.is_lt, float(W1), ALU.mult)
+    ts(C("cf", 17), C("ci", 2), C("cf", 16), ALU.mult, -2.0 * W1, ALU.add)
+    lin(C("cf", 18), blk, 32.0, 2.0 * W1 - 128)
+    lin(V("cf", 22, 24), V("nat", 0, 2), 0.0, C("cf", 18))
+    lin(V("cf", 20, 22), V("cf", 22, 24), 1.0, C("cf", 17))
+    iota(V("xb"), [[1, 5], [0, 32]], 0)
+    ts(V("cm0"), V("xb"), blk, ALU.is_equal, 0.5, ALU.subtract)
+    lin(V("cm"), V("cm0"), 2.0e29)
+    c2, c3 = V("cw", 48, 64), V("cw", 64, 74)
+    iota(c2, [[32, 8], [0, 2]], 0)
+    iota(c3, [[16, 5], [0, 2]], W1 - 256)
+    iota(V("ci", 16, 24), [[16, 8]], 0)
+    cp(V("cu", 16, 24), V("ci", 16, 24))
+    quant(V("uq"), V("us"), V("ub"))
+    op({"v": 50 + ga * 128}, [V("uq"), V("cu", 16, 24)], [V("uq2")],
+       lambda q, T, e: q.tensor_copy(T.uq2[:, 0:128].bitcast(dt.uint32), T.uq[:, 0:128].bitcast(dt.uint32).indirect(T.cu[:, 16:24])))
+    op({"s": 65 + ga * 128}, [V("us"), V("cu", 16, 24)], [V("us2")],
+       lambda q, T, e: q.activation(T.us2[:, 0:128], T.us[:, 0:128].indirect(T.cu[:, 16:24]), ACT.Copy))
+    quant(V("vq"), V("vs"), V("vb"))
+    iota(V("e16"), [[0, 128]], 16)
+    iota(V("eb"), [[0, 2048]], 0)
+    for b in range(4):
+        select(V("eb", 513 * b, 512 * b + 512, 4), V("e16"), [[-1, 128]], 0, 1, 0.0)
+    quant(V("eq"), V("es"), V("eb"))
+    for hf in range(2):
+        quant(V("landq", 368 * hf, 368 * hf + 128), V("lands", 368 * hf, 368 * hf + 128), V("x_%d" % hf, 0, 512))
+        fill(V("pt", 1152 * hf, 1152 * hf + 192), 0.0)
+
+    def tree(hf):
+        h = "_%d" % hf
+        now[0] = hf
+        ls = lambda k, n=10: V("ls" + h, 12 * k, 12 * k + n)
+        fr = lambda k: V("fr" + h, W1 * k, W1 * k + H)
+        tb = lambda k: V("tb" + h, H * k, H * k + H)
+        sm = lambda k: V("sm" + h, 16 * k, 16 * k + 10)
+        si = lambda k: V("si" + h, 16 * k, 16 * k + 10)
+        fill(V("ls" + h), END)
+        for b in range(4):
+            fill(V("win" + h, 256 * b + H, 256 * b + W1), 0.0)
+            fill(V("xh" + h, 336 * b + H, 336 * b + W1), 0.0)
+        ts(ls(0), V("fnb", 10 * hf, 10 * hf + 10), float(H * hf), ALU.subtract)
+        lin(fr(0), V("nat", 0, H), idx=ls(0))
+        for k in range(3):
+            lin(fr(k + 1), fr(k), idx=ls(0))
+        wrap(ls(1), fr(3), tb(0))
+        lin(fr(4), fr(3), idx=ls(1))
+        lin(fr(5), fr(4), idx=ls(1))
+        wrap(ls(2), fr(5), tb(1))
+        lin(fr(7), V("wt"), idx=ls(1))
+        lin(fr(8), fr(7), idx=ls(1))
+        lin(fr(9), fr(8), idx=ls(2))
+        lin(fr(6), fr(9), idx=ls(2))
+        scan(tb(4), V("keep"), fr(6), 0.0, ALU.mult, ALU.min)
+        scan(tb(5), V("keep"), fr(6), 0.0, ALU.mult, ALU.max)
+        cyc = ls(5)
+        ts((cyc[0], cyc[1], cyc[2], 2), (tb(4)[0], tb(4)[1] + 31, tb(4)[2], 32), float(END), ALU.add)
+        ts((cyc[0], cyc[1] + 1, cyc[2], 2), (tb(5)[0], tb(5)[1] + 31, tb(5)[2], 32), -1.0, ALU.mult, float(END), ALU.add)
+        fill(V("fr" + h, H, W1), -65536.0)
+        tt(V("kg" + h), V("fr" + h, 0, W1), V("keyb"), ALU.add, idx=cyc)
+        fill(V("ex" + h, 0, 1), float(H))
+        scan(V("ex" + h, 1, H), V("kg" + h, 0, H - 1), V("cx", 1, H), float(H), ALU.max, ALU.min)
+        scan(V("ex" + h, W1, W1 + H), V("ex" + h, 0, H), V("cvb"), -1.0, ALU.max, ALU.add)
+        ts(sm(0), cyc, float(END), ALU.not_equal)
+        ts(sm(1), cyc, float(END), ALU.is_equal)
+        tt(sm(2), sm(1), iw, ALU.mult)
+        tt(si(0), V("ex" + h, W1 + 15, W1 + H, 16), sm(0), ALU.mult)
+        ts(si(1), si(0), 255, ALU.bitwise_and)
+        tt(sm(3), si(1), sm(2), ALU.add)
+        cp(ls(6), sm(3))
+        up = V("up" + h)
+        fill(up, float(END))
+        op({"v": 50 + par["sc"] * H}, [fr(0), ls(6)], [up], lambda q, T, e: q.tensor_copy(ap(T, up).indirect(ap(T, ls(6))), ap(T, fr(0))))
+        w = lambda name, k: V(name + h, W1 * k, W1 * k + W1)
+        u, wsum, wdup, anc, pre = up, V("w0", 0, W1), V("w0", W1, 2 * W1), V("nat"), V("a0")
+        for k in range(3):
+            wrap(ls(7 + k), (u[0], u[1], u[1] + H, 1), tb(6 + k))
+            lst = ls(7 + k, 11)
+            if k == 2:
+                tt(w("wi", 0), wsum, wdup, ALU.add, idx=lst)
+                lin(w("wa", 1), anc, idx=lst)
+                break
+            for j in range(3):
+                lin(w("ur", 3 * k + j), u, idx=lst)
+                u = w("ur", 3 * k + j)
+            tt(w("wr", 3 * k), wsum, wdup, ALU.add, idx=lst)
+            lin(w("wr", 3 * k + 1), w("wr", 3 * k), idx=lst)
+            tt(w("wr", 3 * k + 2), w("wr", 3 * k + 1), w("wr", 3 * k), ALU.add, idx=lst)
+            wsum, wdup = w("wr", 3 * k + 2), w("wr", 6 + k)
+            dup(wdup, wsum)
+            tt(w("ar", 3 * k), pre, anc, ALU.max, idx=lst)
+            lin(w("ar", 3 * k + 1), w("ar", 3 * k), bias=C("cf", 9 + 2 * k), idx=lst)
+            anc = w("ar", 2) if k == 0 else w("wa", 0)
+            tt(anc, w("ar", 3 * k + 1), w("ar", 3 * k), ALU.max, idx=lst)
+            if k == 0:
+                pre = w("ar", 5)
+                lin(pre, anc, bias=C("cf", 10))
+        wsum = w("wi", 0)
+        ts(w("wk", 1), wsum, 16, ALU.arith_shift_right)
+        ts(w("wk", 0), wsum, 7, ALU.arith_shift_right, 511, ALU.bitwise_and)
+        ts(w("wk", 2), wsum, 127, ALU.bitwise_and)
+        fill(V("ka" + h, 0, 20), -1.0e6)
+        cp(V("kb" + h, 1, 20, 2), ls(7))
+
+    def depth(hf):
+        h = "_%d" % hf
+        t0, t1 = V("tb" + h, 0, H), V("tb" + h, H, 2 * H)
+        cp(t0, V("wk" + h, 2 * W1, 2 * W1 + H))
+        scan(t1, t0, V("cv"), -1.0, ALU.max, ALU.add)
+        e = V("tb" + h, H + 15, 2 * H, 16)
+        fill(V("ck" + h), 0.0)
+        tt(V("ck" + h, 0, 10), c3, e, ALU.subtract)
+        lin(V("ck" + h, 16, 26), e, -1.0, -256.0)
+        fill(V("sa" + h, 0, 30), -1.0e6)
+        fill(V("sc" + h, 0, 30), -1.0e6)
+        lin(V("sc" + h, 2, 30, 3), iw)
+
+    def front(t, hf):
+        h = "_%d" % hf
+        now[0] = hf
+        k = 2 * t + hf
+        bank = 4 * hf
+        X, Z, Z32 = V("x" + h), V("z" + h), V("z32" + h)
+        quant(V("xq" + h), V("xs" + h), X)
+        mm(bank, H, V("uq2"), V("us2"), V("xq" + h), V("xs" + h))
+        for b in range(4):
+            lin(V("xh" + h, 336 * b, 336 * b + H), (X[0], b, 640, 4), 0.5)
+            dup(V("xi" + h, H * b, H * b + H), V("xh" + h, 336 * b, 336 * b + H))
+        M = V("mx" + h)
+        scan(M, V("ps", 512 * bank, 512 * bank + H), V("cm"), -1.0e29, ALU.max, ALU.min)
+        top, cnt = C("sm" + h, 96), C("sm" + h, 100)
+        op({"v": vc(5)}, [M], [top], lambda q, T, e: q.tensor_reduce(ap(T, top), ap(T, (M[0], 31, H, 32)), AxisListType.X, ALU.max))
+        op({"s": par["act"] + 20 + H * cy}, [M, top], [V("junk" + h), cnt],
+           lambda q, T, e: q.activation(ap(T, V("junk" + h)), ap(T, M), ACT.Sign, bias=ap(T, top), scale=-1.0, accum_out=ap(T, cnt)))
+        lr = lambda a, b: V("lr" + h, a, b)
+        ts(lr(0, 4), V("cf", 20, 24), cnt, ALU.add)
+        ts(lr(4, 20), V("wa" + h), C("cf", 12), ALU.subtract, idx=lr(0, 1))
+        rank = V("ka" + h, 1, 20, 2)
+        tt(V("ka" + h, 1, 33, 2), V("wk" + h, 0, 2 * W1), c2, ALU.add, idx=lr(0, 1))
+        lin(V("kb" + h, 0, 20, 2), rank, 1024.0, -1024.0 * (W1 - 1))
+        scan(V("l2" + h, 0, 20), V("ka" + h, 0, 20), V("kb" + h, 0, 20), 0.0, ALU.min, ALU.max)
+        cp(lr(20, 30), V("l2" + h, 1, 20, 2))
+        for b in range(4):
+            lin(V("xh" + h, 336 * b + W1, 336 * b + 336), V("xh" + h, 336 * b, 336 * b + W1), idx=lr(4, 14))
+            tt((Z[0], b, 640, 4), V("xh" + h, 336 * b, 336 * b + 336), V("xi" + h, H * b, H * b + H), ALU.add, idx=lr(20, 30))
+            lin((Z32[0], H * b, H * b + H, 1), (Z[0], b, 640, 4), 32.0)
+        if t == 2:
+            lin(V("pw" + h, 0, W1), V("nat"), 1.0, float(H * hf))
+            lin(V("pw" + h, W1, W1 + H), V("pw" + h, 0, W1), idx=lr(4, 14))
+            lin(V("fob", H * hf, H * hf + H), V("pw" + h), idx=lr(20, 30))
+        quant(V("zq" + h), V("zs" + h), Z)
+        base = 4 * (288 * hf + 48 + 80 * t)
+        for b in range(4):
+            mm(bank + b, H, V("wq", 128 * b, 128 * b + 128), V("wsc", 128 * b, 128 * b + 128), V("zq" + h), V("zs" + h))
+        for b in range(4):
+            tt(V("win" + h, 256 * b, 256 * b + H), V("ps", 512 * (bank + b), 512 * (bank + b) + H), (Z32[0], H * b, H * b + H, 1), ALU.add)
+            lin(V("pt", base + b, base + 320, 4), V("win" + h, 256 * b, 256 * b + W1), 1.0 / 32, idx=lr(14, 19))
+        quant(V("pq", 128 * k, 128 * k + 128), V("psc", 128 * k, 128 * k + 128), V("pt", base - 192, base + 320))
+        a, la = 128 * k + 48, 368 * hf + 128 + 80 * t
+        op({"g": 300.0}, [V("pq", a, a + 80), V("psc", a, a + 80)], [V("landq", la, la + 80), V("lands", la, la + 80)], None,
+           kind="rem", sem="arr%d" % k, lat=par["rem"], step=STEP[t], a=a, la=la)
+        lin(V("p16" + h), V("pt", base, base + 320), 16.0)
+        if t == 0:
+            depth(hf)
+        tt(V("sa" + h, 2, 98, 3), V("wk" + h), V("ck" + h), ALU.add, idx=lr(2, 4))
+        lin(V("sa" + h, 1, 30, 3), V("sa" + h, 50, 80, 3), -1024.0, 16384.0)
+        lin(V("sc" + h, 0, 30, 3), rank, 1024.0, -1024.0 * (W1 - 1))
+        scan(V("sm" + h, 128, 158), V("sa" + h, 0, 30), V("sc" + h, 0, 30), 0.0, ALU.min, ALU.max)
+        cp(lr(70, 80), V("sm" + h, 130, 158, 3))
+
+    def back(t, hf):
+        h = "_%d" % hf
+        now[0] = hf
+        bank = 4 * hf
+        la = 368 * hf + 128 + 80 * t
+        for b in range(4):
+            mm(bank + b, 128, V("eq", 128 * b, 128 * b + 128), V("es", 128 * b, 128 * b + 128), V("landq", la - 48, la + 80), V("lands", la - 48, la + 80))
+        for b in range(4):
+            tt(V("win" + h, 256 * b + W1, 256 * b + 256), V("ps", 512 * (bank + b) + 48, 512 * (bank + b) + 128), V("p16" + h, b, 320, 4), ALU.add)
+            lin(V("x" + h, b, 640, 4), V("win" + h, 256 * b, 256 * b + 256), 1.0 / 32, idx=V("lr" + h, 70, 80))
+
+    def finish(hf):
+        h = "_%d" % hf
+        now[0] = hf
+        a = H * hf
+        quant(V("xq" + h), V("xs" + h), V("x" + h))
+        mm(4 * hf, H, V("vq"), V("vs"), V("xq" + h), V("xs" + h))
+        dma("y", [V("xq" + h)], [], lambda T: (T.oc[:, 4 * a:4 * a + 4 * H], T["xq" + h][:].bitcast(dt.uint8)), "out", 2200.0)
+        for j in range(4):
+            dma("ys"[j % 2], [V("xs" + h)], [], lambda T, j=j: (T.osc[4 * j:4 * j + 4, a:a + H], T["xs" + h][32 * j:32 * j + 4, :]), "out", 2000.0)
+        lin(V("yb", a, a + H), V("ps", 2048 * hf, 2048 * hf + H))
+        dma("y", [V("yb", a, a + H)], [], lambda T: (T.y[:, a:a + H], T.yb[:, a:a + H]), "out", 2200.0)
+
+    for hf in range(2):
+        tree(hf)
+    for t in range(3):
+        for hf in range(2):
+            if t:
+                back(t - 1, hf)
+            front(t, hf)
+    dma("y", [V("fob")], [], lambda T: (T.fo[:], T.fob[0:128:16, :]), "out", 2000.0)
+    for hf in range(2):
+        back(2, hf)
+        finish(hf)
+    return ops
+
+
+def depend(ops):
+    writer = {n: np.full(s[1][1], -1) for n, s in SCRATCH.items()}
+    readers = {n: [] for n in SCRATCH}
+    for i, o in enumerate(ops):
+        dep = set()
+        rd = [a for a in o["rd"] if a[0] != "ps"]
+        wr = [a if a[0] != "ps" else ("ps", a[1] // 512 * 512, a[1] // 512 * 512 + 512, 1) for a in o["wr"] + [a for a in o["rd"] if a[0] == "ps"]]
+        for a in rd + wr:
+            dep.update(int(j) for j in np.unique(writer[a[0]][a[1]:a[2]:a[3]]) if j >= 0)
+        for a in wr:
+            m = np.zeros(len(writer[a[0]]), bool)
+            m[a[1]:a[2]:a[3]] = True
+            dep.update(j for j, b in readers[a[0]] if m[b[1]:b[2]:b[3]].any())
+        for a in rd:
+            readers[a[0]].append((i, a))
+        for a in wr:
+            writer[a[0]][a[1]:a[2]:a[3]] = i
+        dep.discard(i)
+        o["dep"] = sorted(dep)
+
+
+def place(ops, seq, par, pre, eng, bias, back=False):
+    hop, xhop = par["hop"], par["xhop"]
+    line = {e: [] for e in "vspgy"}
+    start, done, out = {}, {}, {}
+    for i in seq:
+        o, best = ops[i], None
+        for e, d in o["dur"].items():
+            if eng[i] is not None and eng[i] != e:
+                continue
+            st = 0.0
+            for j in pre[i]:
+                x = done[j] + (hop if out[j] == e else xhop)
+                if x > st:
+                    st = x
+            if back:
+                st += o.get("lat", 0.0)
+            ln = line[e]
+            k = len(ln)
+            while k > 0 and ln[k - 1][1] > st:
+                k -= 1
+            while k < len(ln) and ln[k][0] < st + d:
+                st = max(st, ln[k][1])
+                k += 1
+            key = st + d * (bias if e == "v" else 1.0)
+            if best is None or key < best[0]:
+                best = (key, st, e, d, k)
+        key, st, e, d, k = best
+        line[e].insert(k, (st, st + d))
+        start[i], done[i], out[i] = st, st + d + (0.0 if back else o.get("lat", 0.0)), e
+    return start, done, out
+
+
+def replay(ops, order, eng, par):
+    free = dict.fromkeys("vspgy", 0.0)
+    done = {}
+    for i in order:
+        e = eng[i]
+        st = free[e]
+        for j in ops[i]["dep"]:
+            x = done[j] + (par["hop"] if eng[j] == e else par["xhop"])
+            if x > st:
+                st = x
+        free[e] = st + ops[i]["dur"][e]
+        done[i] = free[e] + ops[i].get("lat", 0.0)
+    return max(done.values())
+
+
+def arrange(ops, par, others, tries):
+    n = len(ops)
+    pre = [o["dep"] for o in ops]
+    succ = [[] for _ in ops]
+    for i in range(n):
+        for j in pre[i]:
+            succ[j].append(i)
+    tail = [0.0] * n
+    for i in range(n - 1, -1, -1):
+        tail[i] = min(ops[i]["dur"].values()) + ops[i].get("lat", 0.0) + max([tail[j] + par["hop"] for j in succ[i]] + [0.0])
+    x = [12345]
+
+    def rnd():
+        x[0] = (x[0] * 1103515245 + 12345) % 2147483648
+        return x[0] / 2147483648.0
+
+    def legal(pr):
+        pr = list(pr)
+        for i in range(n - 1, -1, -1):
+            for j in succ[i]:
+                if pr[i] >= pr[j]:
+                    pr[i] = pr[j] - 1e-3
+        return sorted(range(n), key=lambda i: (pr[i], i))
+    flex = [i for i in range(n) if len(ops[i]["dur"]) > 1]
+    best, top = None, None
+    for it in range(tries):
+        if it < 40:
+            pr = [-tail[i] + 1000.0 * (it % 10) * ops[i]["hf"] for i in range(n)]
+            bias, fix = 1.0 + 0.7 * (it // 10), [None] * n
+        else:
+            pr, fix, bias = list(best[3]), list(best[2]), 1.0
+            a, w = rnd() * best[4], 300 + 3000 * rnd() * rnd()
+            u = rnd()
+            if u < 0.35:
+                amp = 100 + 1500 * rnd()
+                pr = [s + (amp * (rnd() - 0.5) if a < s < a + w else 0.0) for s in pr]
+            elif u < 0.6:
+                amp, hf = 2000 * (rnd() - 0.5), int(rnd() * 2)
+                pr = [s + (amp if a < s < a + w and ops[i]["hf"] == hf else 0.0) for i, s in enumerate(pr)]
+            else:
+                for _ in range(1 + int(rnd() * 2)):
+                    i = flex[int(rnd() * len(flex))]
+                    alt = [e for e in ops[i]["dur"] if e != fix[i]]
+                    fix[i] = alt[int(rnd() * len(alt))]
+        start, done, eng = place(ops, legal(pr), par, pre, fix, bias)
+        if it < 40 or it % JUST == 0:
+            fix = [eng[i] for i in range(n)]
+            s2, d2, e2 = place(ops, legal([start[i] + ops[i]["dur"][eng[i]] for i in range(n)])[::-1], par, succ, fix, 1.0, True)
+            start, done, eng = place(ops, legal([-d2[i] for i in range(n)]), par, pre, fix, 1.0)
+        order = sorted(range(n), key=lambda i: (start[i], i))
+        cost = sum(replay(q, order, eng, p) for q, p in others) / len(others)
+        if best is None or cost <= best[0] + (0.0 if it < 40 else TEMP * (1.0 - it / tries)):
+            best = (cost, order, [eng[i] for i in range(n)], [start[i] for i in range(n)], max(done.values()), [done[i] for i in range(n)])
+            if top is None or cost < top[0]:
+                top = best
+    return top[1], top[2], top[5], top[0]
+
+
+def plan(tries):
+    sets = []
+    for ch in ({}, {"cy": 0.85, "g": 0.95, "sc": 1.6, "hop": 50.0, "xhop": 80.0, "rem": 2500.0}, {"cy": 1.2, "g": 1.7, "sc": 4.8, "hop": 100.0, "xhop": 150.0, "rem": 4500.0},
+               {"cy": 1.2, "g": 1.0, "hop": 120.0, "xhop": 200.0}):
+        p = dict(PAR)
+        p.update(ch)
+        q = build(p)
+        depend(q)
+        sets.append((q, p))
+    return (sets[0][0],) + arrange(sets[0][0], PAR, sets, tries)
+
+
+OPS, ORDER, ENG, DONE, COST = plan(TRIES)
+
+
+def rank_program(g, core, T, topo):
+    rank = T.rank_of(core)
+    if rank is None:
+        return
+    queue = {"v": g.vector, "s": g.scalar, "p": g.tensor, "g": g, "y": g.sync}
+    count = dict.fromkeys(["v", "s", "p", "g", "out", "sent"], 0)
+    mark, known = {}, {}
+    seen = {e: {} for e in queue}
+    for i in ORDER:
+        o, e = OPS[i], ENG[i]
+        q = queue[e]
+        for j in sorted(o["dep"], key=lambda j: -DONE[j]):
+            s, c = mark[j]
+            if seen[e].get(s, 0) < c:
+                q.wait_ge(T.sem[s], c)
+                seen[e][s] = c
+                for s2, c2 in known[j].items():
+                    seen[e][s2] = max(seen[e].get(s2, 0), c2)
+        known[i] = dict(seen[e])
+        if o["kind"] == "c":
+            o["emit"](q, T, e).then_inc(T.sem[e], 1)
+            count[e] += 1
+            mark[i] = (e, count[e])
+        elif o["kind"] == "dma":
+            o["emit"](q, T, e).then_inc(T.sem[o["sem"]], 16)
+            count[o["sem"]] = count.get(o["sem"], 0) + 16
+            mark[i] = (o["sem"], count[o["sem"]])
+        else:
+            peer = T.cores[rank ^ o["step"]]
+            rid, pid = topo.addr(peer, core)
+            m, n = topo.mask(core, peer), len(topo.engines(core, peer))
+            a, la = o["a"], o["la"]
+            g.remote_dma(T.landq[:, la:la + 80].bitcast(dt.uint8), T.pq[:, a:a + 80].bitcast(dt.uint8), T.sem[o["sem"]], T.sem.sent, pid, rid, m)
+            g.remote_dma(T.lands[:, la:la + 80], T.psc[:, a:a + 80], T.sem[o["sem"]], T.sem.sent, pid, rid, m)
+            count["sent"] += 2 * n
+            mark[i] = (o["sem"], 2 * n)
+            known[i] = {}
+    for s in ("g", "sent", "v", "s", "p", "out"):
+        g.wait_ge(T.sem[s], count[s])

@@ -28,8 +28,12 @@ SCRATCH["ps"] = ("psum", [128, 4096], F32)
 
 SEMAPHORES = ["v", "s", "p", "g", "sent", "out"] + ["ld%d" % k for k in range(7)] + ["arr%d" % k for k in range(6)]
 
-PAR = {"cy": 1.0, "g": 1.3, "sc": 3.2, "hop": 70.0, "xhop": 110.0, "load": 2300.0, "rem": 3200.0, "act": 65.0}
-TRIES, JUST, TEMP = 6000, 2, 40.0
+PAR = {"cy": 1.0, "g": 1.4, "sc": 3.2, "hop": 130.0, "xhop": 170.0, "load": 2500.0, "rem": 3600.0, "act": 90.0, "iss": 600.0, "fx": 20.0, "dq": 200.0}
+SETS = [{}, {"hop": 175.0, "xhop": 175.0, "g": 1.3, "rem": 3200.0, "act": 65.0, "iss": 300.0, "fx": 0.0, "dq": 60.0},
+        {"hop": 70.0, "xhop": 110.0, "g": 1.3, "rem": 5500.0, "act": 65.0, "iss": 1000.0, "fx": 0.0, "dq": 400.0},
+        {"hop": 70.0, "xhop": 110.0, "g": 1.3, "rem": 3200.0, "act": 150.0, "iss": 300.0, "fx": 60.0},
+        {"hop": 40.0, "xhop": 260.0, "g": 1.3, "rem": 3200.0, "act": 65.0, "iss": 300.0, "fx": 0.0}]
+TRIES, JUST, TEMP = 9000, 2, 40.0
 
 
 def size(a):
@@ -66,7 +70,7 @@ def build(par):
         ops.append(dict(hf=now[0], dur=dur, rd=views(*rd), wr=views(*wr), emit=emit, kind=kind, **kw))
 
     def vc(n):
-        return max(n, 64) * cy
+        return max(n * cy + par["fx"], 64 * cy)
 
     def ts(out, a, s1, op0, s2=None, op1=None, idx=None):
         def emit(q, T, e):
@@ -141,7 +145,7 @@ def build(par):
         op({"p": (n + 16) * 1.1}, [lq, lsc, rq, rsc], [out], lambda q, T, e: q.matmul_mx(ap(T, out), ap(T, lq), ap(T, lsc), ap(T, rq), ap(T, rsc), True, True))
 
     def dma(eng, rd, wr, f, sem, lat):
-        op({eng: 60.0}, rd, wr, lambda q, T, e: q.dma_start(*f(T)), kind="dma", sem=sem, lat=lat)
+        op({e: par["dq"] for e in eng}, rd, wr, lambda q, T, e: q.dma_start(*f(T)), kind="dma", sem=sem, lat=lat)
 
     def wrap(lst, rep, tmp):
         scan(tmp, rep, V("cv"), -1.0, ALU.max, ALU.add)
@@ -163,10 +167,10 @@ def build(par):
     ts(ri, C("ci", 0), 15, ALU.bitwise_and)
     cp(rf, ri)
     lin(r16, rf, 1.0, 16.0)
-    ts(C("cf", 2), ri, -512.0, ALU.mult, 256.0, ALU.add)
-    ts(C("cf", 3), ri, -16.0, ALU.mult, 240.0, ALU.add)
+    lin(C("cf", 2), rf, -512.0, 256.0)
+    lin(C("cf", 3), rf, -16.0, 240.0)
     ts(C("cf", 4), C("cf", 3), C("cf", 3), ALU.mult, 256.0, ALU.add)
-    ts(V("cv"), V("tm16"), C("cf", 2), ALU.add)
+    lin(V("cv"), V("tm16"), 1.0, C("cf", 2))
     ts(V("cv", 15, H, 16), V("tm16", 0, H, 16), C("cf", 4), ALU.subtract)
     lin(V("cvb"), V("cv"), 256.0, eng="s")
     iota(V("xl"), [[0, 5], [1, 32]], 0)
@@ -184,11 +188,11 @@ def build(par):
     select(V("cx"), V("cx0"), [[0, 5], [1, 32]], 0, 0, 1.0e6)
     iota(V("cw", 16, 26), [[16, 10]], 0)
     iw = V("cw", 32, 42)
-    ts(iw, V("cw", 16, 26), rf, ALU.add)
+    lin(iw, V("cw", 16, 26), 1.0, rf)
     ts(V("s32", 96, 128), nat32, rf, ALU.is_lt, 128.0, ALU.mult)
     ts(V("s32", 128, 160), nat32, r16, ALU.is_lt, 65536.0, ALU.mult)
-    ts(V("s32", 160, 192), V("s32", 32, 64), 128.0 * W1, ALU.mult, 1.0, ALU.add)
-    ts(V("s32", 192, 224), V("s32", 0, 32), 65536.0 * W1, ALU.mult)
+    ts(V("s32", 160, 192), V("s32", 32, 64), 128.0 * (W1 + 32), ALU.mult, 1.0, ALU.add)
+    ts(V("s32", 192, 224), V("s32", 0, 32), 65536.0 * (W1 + 32), ALU.mult)
     tt(V("s32", 96, 160), V("s32", 96, 160), V("s32", 160, 224), ALU.add)
     tt(V("s32", 224, 256), V("s32", 96, 128), V("s32", 128, 160), ALU.add)
     lin(V("w0", 0, H), V("s32", 224, 256), idx=V("cu", 0, 10))
@@ -213,7 +217,7 @@ def build(par):
     ts(V("cm0"), V("xb"), blk, ALU.is_equal, 0.5, ALU.subtract)
     lin(V("cm"), V("cm0"), 2.0e29)
     c2, c3 = V("cw", 48, 64), V("cw", 64, 74)
-    iota(c2, [[32, 8], [0, 2]], 0)
+    iota(c2, [[32, 8], [0, 2]], -32)
     iota(c3, [[16, 5], [0, 2]], W1 - 256)
     iota(V("ci", 16, 24), [[16, 8]], 0)
     cp(V("cu", 16, 24), V("ci", 16, 24))
@@ -304,8 +308,7 @@ def build(par):
         ts(w("wk", 1), wsum, 16, ALU.arith_shift_right)
         ts(w("wk", 0), wsum, 7, ALU.arith_shift_right, 511, ALU.bitwise_and)
         ts(w("wk", 2), wsum, 127, ALU.bitwise_and)
-        fill(V("ka" + h, 0, 20), -1.0e6)
-        cp(V("kb" + h, 1, 20, 2), ls(7))
+        cp(V("kb" + h, 0, 10), ls(7))
 
     def depth(hf):
         h = "_%d" % hf
@@ -340,11 +343,10 @@ def build(par):
         lr = lambda a, b: V("lr" + h, a, b)
         ts(lr(0, 4), V("cf", 20, 24), cnt, ALU.add)
         ts(lr(4, 20), V("wa" + h), C("cf", 12), ALU.subtract, idx=lr(0, 1))
-        rank = V("ka" + h, 1, 20, 2)
-        tt(V("ka" + h, 1, 33, 2), V("wk" + h, 0, 2 * W1), c2, ALU.add, idx=lr(0, 1))
-        lin(V("kb" + h, 0, 20, 2), rank, 1024.0, -1024.0 * (W1 - 1))
-        scan(V("l2" + h, 0, 20), V("ka" + h, 0, 20), V("kb" + h, 0, 20), 0.0, ALU.min, ALU.max)
-        cp(lr(20, 30), V("l2" + h, 1, 20, 2))
+        rank = V("ka" + h, 0, 10)
+        tt(V("ka" + h, 0, 16), V("wk" + h, 0, 2 * W1), c2, ALU.add, idx=lr(0, 1))
+        tt(V("l2" + h, 0, 10), rank, V("kb" + h, 0, 10), ALU.max)
+        cp(lr(20, 30), V("l2" + h, 0, 10))
         for b in range(4):
             lin(V("xh" + h, 336 * b + W1, 336 * b + 336), V("xh" + h, 336 * b, 336 * b + W1), idx=lr(4, 14))
             tt((Z[0], b, 640, 4), V("xh" + h, 336 * b, 336 * b + 336), V("xi" + h, H * b, H * b + H), ALU.add, idx=lr(20, 30))
@@ -362,7 +364,7 @@ def build(par):
             lin(V("pt", base + b, base + 320, 4), V("win" + h, 256 * b, 256 * b + W1), 1.0 / 32, idx=lr(14, 19))
         quant(V("pq", 128 * k, 128 * k + 128), V("psc", 128 * k, 128 * k + 128), V("pt", base - 192, base + 320))
         a, la = 128 * k + 48, 368 * hf + 128 + 80 * t
-        op({"g": 300.0}, [V("pq", a, a + 80), V("psc", a, a + 80)], [V("landq", la, la + 80), V("lands", la, la + 80)], None,
+        op({"g": par["iss"]}, [V("pq", a, a + 80), V("psc", a, a + 80)], [V("landq", la, la + 80), V("lands", la, la + 80)], None,
            kind="rem", sem="arr%d" % k, lat=par["rem"], step=STEP[t], a=a, la=la)
         lin(V("p16" + h), V("pt", base, base + 320), 16.0)
         if t == 0:
@@ -390,11 +392,11 @@ def build(par):
         a = H * hf
         quant(V("xq" + h), V("xs" + h), V("x" + h))
         mm(4 * hf, H, V("vq"), V("vs"), V("xq" + h), V("xs" + h))
-        dma("y", [V("xq" + h)], [], lambda T: (T.oc[:, 4 * a:4 * a + 4 * H], T["xq" + h][:].bitcast(dt.uint8)), "out", 2200.0)
+        dma("ys", [V("xq" + h)], [], lambda T: (T.oc[:, 4 * a:4 * a + 4 * H], T["xq" + h][:].bitcast(dt.uint8)), "out", 2200.0)
         for j in range(4):
-            dma("ys"[j % 2], [V("xs" + h)], [], lambda T, j=j: (T.osc[4 * j:4 * j + 4, a:a + H], T["xs" + h][32 * j:32 * j + 4, :]), "out", 2000.0)
+            dma("ys", [V("xs" + h)], [], lambda T, j=j: (T.osc[4 * j:4 * j + 4, a:a + H], T["xs" + h][32 * j:32 * j + 4, :]), "out", 2000.0)
         lin(V("yb", a, a + H), V("ps", 2048 * hf, 2048 * hf + H))
-        dma("y", [V("yb", a, a + H)], [], lambda T: (T.y[:, a:a + H], T.yb[:, a:a + H]), "out", 2200.0)
+        dma("ys", [V("yb", a, a + H)], [], lambda T: (T.y[:, a:a + H], T.yb[:, a:a + H]), "out", 2200.0)
 
     for hf in range(2):
         tree(hf)
@@ -538,8 +540,7 @@ def arrange(ops, par, others, tries):
 
 def plan(tries):
     sets = []
-    for ch in ({}, {"cy": 0.85, "g": 0.95, "sc": 1.6, "hop": 50.0, "xhop": 80.0, "rem": 2500.0}, {"cy": 1.2, "g": 1.7, "sc": 4.8, "hop": 100.0, "xhop": 150.0, "rem": 4500.0},
-               {"cy": 1.2, "g": 1.0, "hop": 120.0, "xhop": 200.0}):
+    for ch in SETS:
         p = dict(PAR)
         p.update(ch)
         q = build(p)

@@ -28,12 +28,10 @@ SCRATCH["ps"] = ("psum", [128, 4096], F32)
 
 SEMAPHORES = ["v", "s", "p", "g", "sent", "out"] + ["ld%d" % k for k in range(7)] + ["arr%d" % k for k in range(6)]
 
-PAR = {"cy": 1.0, "g": 1.4, "sc": 3.2, "hop": 130.0, "xhop": 170.0, "load": 2500.0, "rem": 3600.0, "act": 90.0, "iss": 600.0, "fx": 20.0, "dq": 200.0}
-SETS = [{}, {"hop": 175.0, "xhop": 175.0, "g": 1.3, "rem": 3200.0, "act": 65.0, "iss": 300.0, "fx": 0.0, "dq": 60.0},
-        {"hop": 70.0, "xhop": 110.0, "g": 1.3, "rem": 5500.0, "act": 65.0, "iss": 1000.0, "fx": 0.0, "dq": 400.0},
-        {"hop": 70.0, "xhop": 110.0, "g": 1.3, "rem": 3200.0, "act": 150.0, "iss": 300.0, "fx": 60.0},
-        {"hop": 40.0, "xhop": 260.0, "g": 1.3, "rem": 3200.0, "act": 65.0, "iss": 300.0, "fx": 0.0}]
-TRIES, JUST, TEMP = 9000, 2, 40.0
+PAR = {"cy": 1.04, "g": 1.3, "sc": 3.2, "hop": 175.0, "xhop": 175.0, "load": 2500.0, "rem": 3300.0, "act": 65.0, "iss": 300.0, "fx": 0.0, "dq": 100.0}
+SETS = [{}, {"cy": 0.85, "g": 1.0, "sc": 1.8, "hop": 190.0, "xhop": 190.0},
+        {"cy": 1.2, "g": 1.7, "sc": 4.5, "hop": 200.0, "xhop": 200.0, "rem": 4500.0, "iss": 600.0}]
+TRIES, JUST, TEMP = 12000, 1, 100.0
 
 
 def size(a):

@@ -10,28 +10,39 @@ BF, F32, I32, U16, CODE, U8 = "bfloat16", "float32", "int32", "uint16", "float8_
 SCRATCH = {}
 for _n, _w, _d in [
         ("fnb", 20, I32), ("ub", 512, BF), ("vb", 512, BF), ("uq", 128, CODE), ("us", 128, U8), ("uq2", 128, CODE), ("us2", 128, U8),
-        ("vq", 128, CODE), ("vs", 128, U8), ("wq", 512, CODE), ("wsc", 512, U8), ("eb", 2048, BF), ("e16", 128, BF), ("eq", 512, CODE), ("es", 512, U8),
-        ("landq", 736, CODE), ("lands", 736, U8), ("pq", 768, CODE), ("psc", 768, U8), ("pt", 8 * 288, BF),
-        ("ci", 64, I32), ("cf", 64, F32), ("nat", W1, BF), ("tm16", H, BF), ("xl", H, BF), ("xb", H, BF), ("rev", H, BF),
-        ("keyb", H, F32), ("cx0", H, F32), ("cx", H, F32), ("cv", H, BF), ("cvb", H, F32), ("wt", H, BF), ("w0", 2 * W1, F32), ("a0", W1, F32),
-        ("keep", H, BF), ("cm0", H, BF), ("cm", H, BF), ("s32", 256, F32), ("cw", 80, F32), ("cu", 32, U16), ("fob", 320, F32), ("yb", 320, F32)]:
+        ("vq", 128, CODE), ("vs", 128, U8), ("wq", 512, CODE), ("wsc", 512, U8), ("eb", 2048, BF), ("e16", 128, BF), ("e0", 516, BF), ("eq", 512, CODE), ("es", 512, U8),
+        ("landq", 576, CODE), ("lands", 576, U8), ("pq", 768, CODE), ("psc", 768, U8), ("pt", 8 * 288, BF),
+        ("ci", 64, I32), ("cf", 64, F32), ("nat", W1 + 2, BF), ("natn", H, BF), ("tm16", H, BF), ("xl", H, BF), ("xb", H, BF),
+        ("cv", H, BF), ("wt", H, BF), ("w0", 2 * W1, F32), ("a0", W1, BF), ("ta", 32, F32),
+        ("keep", H, BF), ("w1", H, F32), ("cm", H, BF), ("s32", 320, F32), ("cw", 80, F32), ("cu", 32, U16), ("fob", 320, F32), ("yb", 320, F32)]:
     SCRATCH[_n] = ("sbuf", [128, _w], _d)
 for _h in "01":
     for _n, _w, _d in [
             ("x", 640, BF), ("xh", 4 * 336, BF), ("ka", 40, F32), ("kb", 24, F32), ("z", 640, BF), ("xi", 640, BF), ("z32", 640, BF), ("win", 1024, BF), ("p16", 320, BF),
             ("xq", H, CODE), ("xs", H, U8), ("zq", H, CODE), ("zs", H, U8),
-            ("fr", 10 * W1, BF), ("tb", 12 * H, BF), ("ls", 16 * 12, U16), ("sa", 112, F32), ("sc", 32, F32), ("kg", H, F32), ("ex", 2 * H + 16, F32),
-            ("up", W1, BF), ("pw", W1 + H, F32), ("ur", 6 * W1, BF), ("wr", 8 * W1, F32), ("wi", W1, I32), ("ar", 6 * W1, F32), ("wa", 2 * W1, F32),
-            ("wk", 3 * W1, I32), ("sm", 256, F32), ("si", 32, I32), ("ck", 32, F32), ("mx", H, F32), ("junk", H, BF), ("lr", 96, U16), ("l2", 32, F32)]:
+            ("fr", 12 * W1, BF), ("tb", 12 * H, BF), ("ls", 16 * 12, U16), ("sa", 112, F32), ("sc", 32, F32), ("av", W1, BF), ("nx", W1, BF), ("tc", 64, F32),
+            ("up", W1 + H, BF), ("pw", W1 + H, F32), ("ur", 6 * W1, BF), ("wr", 12 * W1, F32), ("wi", W1, I32), ("ar", 10 * W1, BF), ("wa", 2 * W1, BF),
+            ("wk", 3 * W1, I32), ("mk", 2 * H, F32), ("si", 32, I32), ("sm", 256, F32), ("ck", 32, F32), ("mx", H, F32), ("junk", H, BF), ("lr", 96, U16)]:
         SCRATCH[_n + "_" + _h] = ("sbuf", [128, _w], _d)
 SCRATCH["ps"] = ("psum", [128, 4096], F32)
 
-SEMAPHORES = ["v", "s", "p", "g", "sent", "out"] + ["ld%d" % k for k in range(7)] + ["arr%d" % k for k in range(6)]
+SEMAPHORES = ["v", "s", "p", "g", "sent", "out"] + ["ld%d" % k for k in range(15)] + ["arr%d" % k for k in range(6)]
+SEMAPHORES += ["cp%d" % k for k in range(8)] + ["sel%d" % k for k in range(6)] + ["cw"] + ["dw%d" % k for k in range(8)]
+ADMAS = (4, 4)
+MARK0 = (1,)
+FRADIX, FSTEPS = [4, 3], [1, 1, 2, 2]
+SAME = False
+XDMA = True
+RADIX = [4, 4]
 
-PAR = {"cy": 1.04, "g": 1.3, "sc": 3.2, "hop": 175.0, "xhop": 175.0, "load": 2500.0, "rem": 3300.0, "act": 65.0, "iss": 300.0, "fx": 0.0, "dq": 100.0}
-SETS = [{}, {"cy": 0.85, "g": 1.0, "sc": 1.8, "hop": 190.0, "xhop": 190.0},
-        {"cy": 1.2, "g": 1.7, "sc": 4.5, "hop": 200.0, "xhop": 200.0, "rem": 4500.0, "iss": 600.0}]
-TRIES, JUST, TEMP = 12000, 1, 100.0
+PAR = {"cy": 1.04, "g": 1.3, "sc": 3.2, "hop": 175.0, "xhop": 175.0, "load": 2500.0, "rem": 3300.0, "act": 65.0, "iss": 300.0, "fx": 0.0, "dq": 100.0, "loc": 1900.0, "first": 1500.0}
+SETS = [{}, {"cy": 0.85, "g": 1.0, "sc": 1.8, "hop": 190.0, "first": 800.0, "loc": 2200.0},
+        {"cy": 1.2, "g": 1.7, "sc": 4.5, "hop": 200.0, "rem": 4500.0, "iss": 600.0, "first": 2500.0},
+        {"g": 1.6, "load": 1700.0, "rem": 2600.0, "loc": 1400.0, "first": 1500.0}]
+TRIES = 4000
+MOVES, TEMP2 = 22000, 60.0
+AGAIN = 3
+JUST, TEMP, SEED, MIX = 1, 100.0, 1, (0.5, 0.65, 0.8)
 
 
 def size(a):
@@ -64,8 +75,9 @@ def build(par):
     ops, now = [], [0]
     cy, ga = par["cy"], par["g"]
 
-    def op(dur, rd, wr, emit, kind="c", **kw):
-        ops.append(dict(hf=now[0], dur=dur, rd=views(*rd), wr=views(*wr), emit=emit, kind=kind, **kw))
+    def op(dur, rd, wr, emit, kind="c", lat=0.0, **kw):
+        lat = {e: (lat.get(e, 0.0) if isinstance(lat, dict) else lat) for e in dur}
+        ops.append(dict(hf=now[0], dur=dur, lat=lat, rd=views(*rd), wr=views(*wr), emit=emit, kind=kind, **kw))
 
     def vc(n):
         return max(n * cy + par["fx"], 64 * cy)
@@ -94,36 +106,45 @@ def build(par):
             x = ap(T, a) if idx is None else ap(T, a).indirect(ap(T, idx))
             if e == "s":
                 if isinstance(bias, float) and bias == 0.0:
+                    if isinstance(scale, tuple):
+                        return q.activation(ap(T, out), x, ACT.Identity, scale=ap(T, scale))
                     return q.activation(ap(T, out), x, ACT.Copy, scale=scale) if scale != 1.0 else q.activation(ap(T, out), x, ACT.Copy)
-                return q.activation(ap(T, out), x, ACT.Identity, bias=ap(T, bias), scale=scale)
+                return q.activation(ap(T, out), x, ACT.Identity, bias=ap(T, bias), scale=ap(T, scale))
             if isinstance(bias, float) and bias == 0.0:
-                return q.tensor_scalar(ap(T, out), x, scale, None, ALU.mult) if scale != 1.0 else q.tensor_copy(ap(T, out), x)
-            return q.tensor_scalar(ap(T, out), x, scale, ap(T, bias), ALU.mult, ALU.add)
+                return q.tensor_scalar(ap(T, out), x, ap(T, scale), None, ALU.mult) if scale != 1.0 else q.tensor_copy(ap(T, out), x)
+            return q.tensor_scalar(ap(T, out), x, ap(T, scale), ap(T, bias), ALU.mult, ALU.add)
         n = size(out)
         if idx is None:
             d = {"v": vc(n * (0.5 if two(out, a) else 1)), "s": par["act"] + n * cy}
         else:
             d = {"v": 50 + ga * n, "s": 65 + ga * n}
-        op({e: d[e] for e in eng}, [a, bias, idx], [out], emit)
+        op({e: d[e] for e in eng}, [a, scale, bias, idx], [out], emit)
 
-    def dup(out, a):
+    def dup(out, a, sem=None):
         n = size(out)
 
         def emit(q, T, e):
+            if e == "y":
+                return q.dma_start(ap(T, out), ap(T, a))
             if e == "g":
                 return q.affine_select(ap(T, out), ap(T, a), [[0, n]], ALU.is_equal, 0.0, 0, 0)
             return q.tensor_copy(ap(T, out), ap(T, a)) if e == "v" else q.activation(ap(T, out), ap(T, a), ACT.Copy)
-        op({"v": vc(n * (0.5 if two(out, a) else 1)), "s": par["act"] + n * cy, "g": 170 + 2 * cy * n}, [a], [out], emit)
+        d = {"v": vc(n * (0.5 if two(out, a) else 1)), "s": par["act"] + n * cy, "g": 170 + 2 * cy * n}
+        if sem:
+            d["y"] = par["dq"]
+        op(d, [a], [out], emit, lat={"y": par["loc"]}, sem=sem)
 
     def scan(out, d0, d1, init, op0, op1):
         op({"v": vc(size(out) * (0.5 if two(out, d0, d1) else 1))}, [d0, d1], [out],
            lambda q, T, e: q.tensor_tensor_scan(ap(T, out), ap(T, d0), ap(T, d1), init, op0, op1))
 
-    def fill(out, c):
+    def fill(out, c, eng="vg"):
         d = {"v": vc(size(out) * (0.5 if two(out) else 1))}
         if SCRATCH[out[0]][2] != U16:
             d["g"] = 130 + 2 * cy * size(out)
-        op(d, [], [out], lambda q, T, e: q.memset(ap(T, out), c) if e == "v" else q.iota(ap(T, out), [[0, size(out)]], int(c), 0, allow_small_or_imprecise_dtypes=True))
+        d = {e: d[e] for e in eng if e in d}
+        op(d, [], [out], lambda q, T, e: q.memset(ap(T, out), c) if e == "v" else
+           (q.iota(ap(T, out), [[0, size(out)]], int(c), 0) if SCRATCH[out[0]][2] == I32 else q.iota(ap(T, out), [[0, size(out)]], int(c), 0, allow_small_or_imprecise_dtypes=True)))
 
     def iota(out, pat, base, cm=0):
         def emit(q, T, e):
@@ -146,8 +167,8 @@ def build(par):
         op({e: par["dq"] for e in eng}, rd, wr, lambda q, T, e: q.dma_start(*f(T)), kind="dma", sem=sem, lat=lat)
 
     def wrap(lst, rep, tmp):
-        scan(tmp, rep, V("cv"), -1.0, ALU.max, ALU.add)
-        ts(lst, (tmp[0], tmp[1] + 15, tmp[2], 16), 256.0, ALU.add)
+        scan(tmp, rep, V("cv"), 1.0, ALU.min, ALU.subtract)
+        ts(lst, (tmp[0], tmp[1] + 15, tmp[2], 16), -1.0, ALU.mult, 255.0, ALU.add)
 
     L = par["load"]
     dma("y", [], [V("fnb")], lambda T: (T.fnb[:], T.fn[:]), "ld0", L - 300)
@@ -160,7 +181,7 @@ def build(par):
 
     ri, rf, r16 = C("ci", 1), C("cf", 0), C("cf", 1)
     iota(C("ci", 0), [[0, 1]], 0, 1)
-    iota(V("nat"), [[1, W1]], 0)
+    iota(V("nat"), [[1, W1 + 2]], 0)
     iota(V("tm16"), [[0, 10], [512, 16]], 0)
     ts(ri, C("ci", 0), 15, ALU.bitwise_and)
     cp(rf, ri)
@@ -170,37 +191,42 @@ def build(par):
     ts(C("cf", 4), C("cf", 3), C("cf", 3), ALU.mult, 256.0, ALU.add)
     lin(V("cv"), V("tm16"), 1.0, C("cf", 2))
     ts(V("cv", 15, H, 16), V("tm16", 0, H, 16), C("cf", 4), ALU.subtract)
-    lin(V("cvb"), V("cv"), 256.0, eng="s")
+    iota(V("natn"), [[-1, H]], -1)
     iota(V("xl"), [[0, 5], [1, 32]], 0)
-    iota(V("rev"), [[-1, H]], END)
+    ts(C("cf", 5), rf, 0.0, ALU.not_equal)
+    ts(C("cf", 6), C("cf", 5), float(END), ALU.add)
     iota(V("cw", 0, 10), [[0, 5], [16, 2]], 0)
     ts(V("cu", 0, 10), V("cw", 0, 10), rf, ALU.add)
     nat32 = V("nat", 0, 32)
     ts(V("s32", 0, 32), nat32, r16, ALU.is_equal)
     ts(V("s32", 32, 64), nat32, rf, ALU.is_equal)
     tt(V("s32", 64, 96), V("s32", 0, 32), V("s32", 32, 64), ALU.subtract)
-    tt(V("wt"), V("s32", 64, 96), V("rev"), ALU.mult, idx=V("cu", 0, 10))
+    tt(V("wt"), V("s32", 64, 96), V("nat", END + 1, END + 1 - H, -1), ALU.mult, idx=V("cu", 0, 10))
     ts(V("keep"), V("xl"), 1.0, ALU.min)
-    iota(V("keyb"), [[256, H]], 256)
-    iota(V("cx0"), [[1, 5], [0, 32]], H)
-    select(V("cx"), V("cx0"), [[0, 5], [1, 32]], 0, 0, 1.0e6)
     iota(V("cw", 16, 26), [[16, 10]], 0)
     iw = V("cw", 32, 42)
     lin(iw, V("cw", 16, 26), 1.0, rf)
-    ts(V("s32", 96, 128), nat32, rf, ALU.is_lt, 128.0, ALU.mult)
-    ts(V("s32", 128, 160), nat32, r16, ALU.is_lt, 65536.0, ALU.mult)
-    ts(V("s32", 160, 192), V("s32", 32, 64), 128.0 * (W1 + 32), ALU.mult, 1.0, ALU.add)
-    ts(V("s32", 192, 224), V("s32", 0, 32), 65536.0 * (W1 + 32), ALU.mult)
-    tt(V("s32", 96, 160), V("s32", 96, 160), V("s32", 160, 224), ALU.add)
-    tt(V("s32", 224, 256), V("s32", 96, 128), V("s32", 128, 160), ALU.add)
-    lin(V("w0", 0, H), V("s32", 224, 256), idx=V("cu", 0, 10))
+    fill(V("ta", 0, 20), -1.0e6)
+    lin(V("ta", 1, 20, 2), iw, 1.0, float(W1))
+    iota(V("xb"), [[32, 5], [0, 32]], W1 + 32)
+    ts(V("s32", 96, 128), nat32, rf, ALU.is_lt, 64.0, ALU.mult)
+    ts(V("s32", 160, 192), nat32, r16, ALU.is_lt, 32768.0, ALU.mult)
+    lin(V("s32", 128, 160), V("s32", 32, 64), 64.0)
+    lin(V("s32", 192, 224), V("s32", 0, 32), 32768.0)
+    tt(V("s32", 224, 288), V("s32", 96, 160), V("s32", 160, 224), ALU.add)
+    lin(V("s32", 288, 320), V("s32", 224, 256), 1.0, 1.0)
+    tt(V("w1"), V("s32", 256, 288), V("xb"), ALU.mult, idx=V("cu", 0, 10))
+    tt(V("w0", 0, H), V("s32", 288, 320), V("w1"), ALU.add, idx=V("cu", 0, 10))
     fill(V("w0", H, W1), 0.0)
-    dup(V("w0", W1, 2 * W1), V("w0", 0, W1))
-    for k in range(4):
+    dup(V("w0", W1, 2 * W1), V("w0", 0, W1), "cw")
+    k0 = min(ADMAS) // 2
+    for k in sorted({0} | set(range(k0, 4))):
         ts(C("ci", 2 + k), ri, 1 << k, ALU.bitwise_and)
-        ts(C("cf", 8 + k), C("ci", 2 + k), 256.0 + 8192.0 / (1 << k), ALU.mult, -8192.0, ALU.add)
-    lin(V("a0"), V("nat"), bias=C("cf", 8), eng="s")
-    lin(C("cf", 12), rf, 256.0)
+    ts(V("cf", 8 + k0, 12), V("ci", 2 + k0, 6), 0.0, ALU.is_gt, 256.0, ALU.mult)
+    fill(C("cf", 28), -1.0)
+    ts(V("cf", 24 + k0, 28), V("cf", 8 + k0, 12), -255.0 / 65536, ALU.mult, 1.0, ALU.add)
+    for k in set(ADMAS):
+        op({"v": vc(4)}, [V("cf", 24 + k // 2, 29)], [C("cf", 32 + k)], lambda q, T, e, k=k: q.tensor_reduce(T.cf[:, 32 + k:33 + k], T.cf[:, 24 + k // 2:29], AxisListType.X, ALU.mult))
     ts(C("ci", 6), ri, 1, ALU.arith_shift_right)
     ts(C("cf", 13), ri, 10.0, ALU.is_ge, -8.0, ALU.mult)
     ts(C("cf", 14), ri, -10.0, ALU.add, 4.0, ALU.min)
@@ -211,11 +237,9 @@ def build(par):
     lin(C("cf", 18), blk, 32.0, 2.0 * W1 - 128)
     lin(V("cf", 22, 24), V("nat", 0, 2), 0.0, C("cf", 18))
     lin(V("cf", 20, 22), V("cf", 22, 24), 1.0, C("cf", 17))
-    iota(V("xb"), [[1, 5], [0, 32]], 0)
-    ts(V("cm0"), V("xb"), blk, ALU.is_equal, 0.5, ALU.subtract)
-    lin(V("cm"), V("cm0"), 2.0e29)
-    c2, c3 = V("cw", 48, 64), V("cw", 64, 74)
-    iota(c2, [[32, 8], [0, 2]], -32)
+    lin(C("cf", 19), blk, 32.0, float(W1 + 32))
+    ts(V("cm"), V("xb"), C("cf", 19), ALU.not_equal, -2.0e29, ALU.mult)
+    c3 = V("cw", 64, 74)
     iota(c3, [[16, 5], [0, 2]], W1 - 256)
     iota(V("ci", 16, 24), [[16, 8]], 0)
     cp(V("cu", 16, 24), V("ci", 16, 24))
@@ -226,13 +250,13 @@ def build(par):
        lambda q, T, e: q.activation(T.us2[:, 0:128], T.us[:, 0:128].indirect(T.cu[:, 16:24]), ACT.Copy))
     quant(V("vq"), V("vs"), V("vb"))
     iota(V("e16"), [[0, 128]], 16)
-    iota(V("eb"), [[0, 2048]], 0)
+    iota(V("e0"), [[0, 516]], 0)
+    select(V("e0", 3, 515, 4), V("e16"), [[-1, 128]], 0, 1, 0.0)
     for b in range(4):
-        select(V("eb", 513 * b, 512 * b + 512, 4), V("e16"), [[-1, 128]], 0, 1, 0.0)
+        dma("y", [V("e0")], [V("eb", 512 * b, 512 * b + 512)], lambda T, b=b: (T.eb[:, 512 * b:512 * b + 512], T.e0[:, 3 - b:515 - b]), "ld%d" % (11 + b), 2500.0)
     quant(V("eq"), V("es"), V("eb"))
     for hf in range(2):
-        quant(V("landq", 368 * hf, 368 * hf + 128), V("lands", 368 * hf, 368 * hf + 128), V("x_%d" % hf, 0, 512))
-        fill(V("pt", 1152 * hf, 1152 * hf + 192), 0.0)
+        fill(V("pt", 1152 * hf, 1152 * hf + 192), 0.0, "g")
 
     def tree(hf):
         h = "_%d" % hf
@@ -240,73 +264,115 @@ def build(par):
         ls = lambda k, n=10: V("ls" + h, 12 * k, 12 * k + n)
         fr = lambda k: V("fr" + h, W1 * k, W1 * k + H)
         tb = lambda k: V("tb" + h, H * k, H * k + H)
-        sm = lambda k: V("sm" + h, 16 * k, 16 * k + 10)
-        si = lambda k: V("si" + h, 16 * k, 16 * k + 10)
-        fill(V("ls" + h), END)
-        for b in range(4):
-            fill(V("win" + h, 256 * b + H, 256 * b + W1), 0.0)
-            fill(V("xh" + h, 336 * b + H, 336 * b + W1), 0.0)
-        ts(ls(0), V("fnb", 10 * hf, 10 * hf + 10), float(H * hf), ALU.subtract)
-        lin(fr(0), V("nat", 0, H), idx=ls(0))
-        for k in range(3):
-            lin(fr(k + 1), fr(k), idx=ls(0))
-        wrap(ls(1), fr(3), tb(0))
-        lin(fr(4), fr(3), idx=ls(1))
-        lin(fr(5), fr(4), idx=ls(1))
-        wrap(ls(2), fr(5), tb(1))
-        lin(fr(7), V("wt"), idx=ls(1))
-        lin(fr(8), fr(7), idx=ls(1))
-        lin(fr(9), fr(8), idx=ls(2))
-        lin(fr(6), fr(9), idx=ls(2))
-        scan(tb(4), V("keep"), fr(6), 0.0, ALU.mult, ALU.min)
-        scan(tb(5), V("keep"), fr(6), 0.0, ALU.mult, ALU.max)
-        cyc = ls(5)
-        ts((cyc[0], cyc[1], cyc[2], 2), (tb(4)[0], tb(4)[1] + 31, tb(4)[2], 32), float(END), ALU.add)
-        ts((cyc[0], cyc[1] + 1, cyc[2], 2), (tb(5)[0], tb(5)[1] + 31, tb(5)[2], 32), -1.0, ALU.mult, float(END), ALU.add)
-        fill(V("fr" + h, H, W1), -65536.0)
-        tt(V("kg" + h), V("fr" + h, 0, W1), V("keyb"), ALU.add, idx=cyc)
-        fill(V("ex" + h, 0, 1), float(H))
-        scan(V("ex" + h, 1, H), V("kg" + h, 0, H - 1), V("cx", 1, H), float(H), ALU.max, ALU.min)
-        scan(V("ex" + h, W1, W1 + H), V("ex" + h, 0, H), V("cvb"), -1.0, ALU.max, ALU.add)
-        ts(sm(0), cyc, float(END), ALU.not_equal)
-        ts(sm(1), cyc, float(END), ALU.is_equal)
-        tt(sm(2), sm(1), iw, ALU.mult)
-        tt(si(0), V("ex" + h, W1 + 15, W1 + H, 16), sm(0), ALU.mult)
-        ts(si(1), si(0), 255, ALU.bitwise_and)
-        tt(sm(3), si(1), sm(2), ALU.add)
-        cp(ls(6), sm(3))
         up = V("up" + h)
-        fill(up, float(END))
-        op({"v": 50 + par["sc"] * H}, [fr(0), ls(6)], [up], lambda q, T, e: q.tensor_copy(ap(T, up).indirect(ap(T, ls(6))), ap(T, fr(0))))
-        w = lambda name, k: V(name + h, W1 * k, W1 * k + W1)
-        u, wsum, wdup, anc, pre = up, V("w0", 0, W1), V("w0", W1, 2 * W1), V("nat"), V("a0")
-        for k in range(3):
+        fill(V("ls" + h, 12 * 7 + 10, 12 * 12, 12), END)
+        for b in range(4):
+            fill(V("win" + h, 256 * b + H, 256 * b + W1), 0.0, "g")
+            fill(V("xh" + h, 336 * b + H, 336 * b + W1), 0.0, "g")
+        fill(V("up" + h, H, W1 + H), -float(END + 1), "g")
+        fill(C("up" + h, END + 1), 1.0, "g")
+        fill(C("av" + h, H), -float(END + 1), "g")
+        fill(V("kb" + h, 0, 16), 0.0, "g")
+        ts(ls(0), V("fnb", 10 * hf, 10 * hf + 10), float(H * hf), ALU.subtract)
+        ts(V("tc" + h, 1, 20, 2), V("fnb", 10 * hf, 10 * hf + 10), float(H * hf), ALU.subtract)
+        lin(V("up" + h, 0, H), V("natn", 0, H), idx=ls(0))
+        f, nf = V("up" + h, 0, H), 0
+        for k, rx in enumerate(FRADIX):
+            for j in range(rx - 1):
+                lin(fr(nf), f, idx=ls(k))
+                f = fr(nf)
+                nf += 1
+            wrap(ls(k + 1), f, tb(k))
+        f = V("wt")
+        for k in FSTEPS:
+            lin(fr(nf), f, idx=ls(k))
+            f = fr(nf)
+            nf += 1
+        scan(tb(4), V("keep"), f, 0.0, ALU.mult, ALU.min)
+        scan(tb(5), V("keep"), f, 0.0, ALU.mult, ALU.max)
+        lo, hi = (tb(4)[0], tb(4)[1] + 31, tb(4)[2], 32), (tb(5)[0], tb(5)[1] + 31, tb(5)[2], 32)
+        cyc = ls(5)
+        ts((cyc[0], cyc[1], cyc[2], 2), lo, C("cf", 5), ALU.mult, C("cf", 6), ALU.add)
+        ts((cyc[0], cyc[1] + 1, cyc[2], 2), hi, -1.0, ALU.mult, float(END + 1), ALU.add)
+        lin(V("av" + h, 0, H), V("up" + h, 0, W1), idx=cyc)
+        back_ = V("av" + h, H, 0, -1)
+        scan(V("nx" + h, W1 - 1, W1 - 1 - H, -1), back_, back_, 0.0, ALU.mult, ALU.min)
+        ts(V("tc" + h, 0, 20, 4), lo, 0.0, ALU.is_equal, 1024.0, ALU.mult)
+        ts(V("tc" + h, 2, 20, 4), hi, 0.0, ALU.is_equal, 1024.0, ALU.mult)
+        scan(V("tc" + h, 32, 52), V("ta", 0, 20), V("tc" + h, 0, 20), 0.0, ALU.min, ALU.max)
+        cp(ls(6), V("tc" + h, 33, 52, 2))
+        nx = V("nx" + h, W1 - H, W1)
+        op({"v": 50 + par["sc"] * H}, [nx, ls(6)], [up], lambda q, T, e: q.tensor_copy(ap(T, up).indirect(ap(T, ls(6))), ap(T, nx)))
+        w = lambda name, k, n=W1: V(name + h, W1 * k, W1 * k + n)
+        u, wsum, wdup, anc, pre = V("up" + h, 0, W1), V("w0", 0, W1), V("w0", W1, 2 * W1), w("ar", 0), w("ar", 1)
+        nu, nw, na, bit, ADMA = 0, 0, 2, 0, ADMAS[hf]
+        iota(anc, [[-1, W1]], -1)
+        rows = []
+
+        def pick(m, src):
+            dma("y", [src, anc], [], lambda T: (T["ar" + h][m:128:4, 0:W1], T[src[0]][m:128:4, src[1]:src[2]]), "sel%d" % (3 * hf + m - 1), par["loc"])
+            rows.append(len(ops) - 1)
+        if ADMA:
+            pick(1, u)
+        else:
+            lin(pre, anc, C("cf", 8))
+        for k, rx in enumerate(RADIX + [0]):
             wrap(ls(7 + k), (u[0], u[1], u[1] + H, 1), tb(6 + k))
             lst = ls(7 + k, 11)
-            if k == 2:
-                tt(w("wi", 0), wsum, wdup, ALU.add, idx=lst)
-                lin(w("wa", 1), anc, idx=lst)
+            if rx == 0:
+                tt(w("wi", 0, H), wsum, wdup, ALU.add, idx=ls(7 + k))
+                lin(w("wa", 1, H), anc, idx=ls(7 + k))
                 break
-            for j in range(3):
-                lin(w("ur", 3 * k + j), u, idx=lst)
-                u = w("ur", 3 * k + j)
-            tt(w("wr", 3 * k), wsum, wdup, ALU.add, idx=lst)
-            lin(w("wr", 3 * k + 1), w("wr", 3 * k), idx=lst)
-            tt(w("wr", 3 * k + 2), w("wr", 3 * k + 1), w("wr", 3 * k), ALU.add, idx=lst)
-            wsum, wdup = w("wr", 3 * k + 2), w("wr", 6 + k)
-            dup(wdup, wsum)
-            tt(w("ar", 3 * k), pre, anc, ALU.max, idx=lst)
-            lin(w("ar", 3 * k + 1), w("ar", 3 * k), bias=C("cf", 9 + 2 * k), idx=lst)
-            anc = w("ar", 2) if k == 0 else w("wa", 0)
-            tt(anc, w("ar", 3 * k + 1), w("ar", 3 * k), ALU.max, idx=lst)
-            if k == 0:
-                pre = w("ar", 5)
-                lin(pre, anc, bias=C("cf", 10))
-        wsum = w("wi", 0)
-        ts(w("wk", 1), wsum, 16, ALU.arith_shift_right)
-        ts(w("wk", 0), wsum, 7, ALU.arith_shift_right, 511, ALU.bitwise_and)
-        ts(w("wk", 2), wsum, 127, ALU.bitwise_and)
-        cp(V("kb" + h, 0, 10), ls(7))
+            last = k == len(RADIX) - 1
+            for j in range(rx - 1):
+                short = last and j == rx - 2
+                lin(w("ur", nu, H if short else W1), u, idx=ls(7 + k) if short else lst)
+                u = w("ur", nu)
+                nu += 1
+                if k == 0 and j + 2 < ADMA:
+                    pick(j + 2, u)
+            tt(w("wr", nw), wsum, wdup, ALU.add, idx=lst)
+            wsum = w("wr", nw)
+            nw += 1
+            if (2 << bit) > ADMA:
+                a1 = w("wa", 0) if last and rx == 2 else w("ar", na)
+                tt(a1, pre, anc, ALU.min, idx=lst)
+                ops[-1]["after"] = list(rows)
+                anc = a1
+                na += 1
+            bit += 1
+            if rx == 4:
+                lin(w("wr", nw), wsum, idx=lst)
+                tt(w("wr", nw + 1), w("wr", nw), wsum, ALU.add, idx=lst)
+                wsum = w("wr", nw + 1)
+                nw += 2
+                if (2 << bit) > ADMA:
+                    lin(w("ar", na), anc, C("cf", 8 + bit), idx=lst)
+                    ops[-1]["after"] = list(rows)
+                    a1 = w("wa", 0) if last else w("ar", na + 1)
+                    tt(a1, w("ar", na), anc, ALU.min, idx=lst)
+                    anc = a1
+                    na += 2
+                bit += 1
+            if last:
+                wdup = w("wr", nw, H)
+                dup(wdup, (wsum[0], wsum[1], wsum[1] + H, 1), "dw%d" % (4 * hf + k))
+            else:
+                wdup = w("wr", nw)
+                nw += 1
+                dup(wdup, wsum, "dw%d" % (4 * hf + k))
+                pre = w("ar", na)
+                na += 1
+                lin(pre, anc, C("cf", 8 + bit))
+                ops[-1]["after"] = list(rows)
+        wsum = w("wi", 0, H)
+        ts(w("wk", 1, H), wsum, 15, ALU.arith_shift_right)
+        ts(w("wk", 0, H), wsum, 6, ALU.arith_shift_right, 511, ALU.bitwise_and)
+        ts(w("wk", 2, H), wsum, 63, ALU.bitwise_and)
+        for j in range(3):
+            fill(V("wk" + h, W1 * j + H, W1 * j + W1), 0.0, "g")
+        fill(V("wa" + h, W1 + H, 2 * W1), 0.0, "g")
+        ts(V("kb" + h, 0, 10), ls(7), 32.0, ALU.add)
 
     def depth(hf):
         h = "_%d" % hf
@@ -331,26 +397,39 @@ def build(par):
         mm(bank, H, V("uq2"), V("us2"), V("xq" + h), V("xs" + h))
         for b in range(4):
             lin(V("xh" + h, 336 * b, 336 * b + H), (X[0], b, 640, 4), 0.5)
-            dup(V("xi" + h, H * b, H * b + H), V("xh" + h, 336 * b, 336 * b + H))
+            if not SAME:
+                dup(V("xi" + h, H * b, H * b + H), V("xh" + h, 336 * b, 336 * b + H), "cp%d" % (4 * hf + b) if XDMA else None)
+        if t == 0:
+            dma("y", [V("xq" + h, 0, 48)], [V("landq", 288 * hf, 288 * hf + 48)],
+                lambda T: (T.landq[:, 288 * hf:288 * hf + 48].bitcast(dt.uint8), T["xq" + h][:, 0:48].bitcast(dt.uint8)), "ld%d" % (7 + 2 * hf), 2200.0)
+            dma("y", [V("xs" + h, 0, 48)], [V("lands", 288 * hf, 288 * hf + 48)],
+                lambda T: (T.lands[:, 288 * hf:288 * hf + 48], T["xs" + h][:, 0:48]), "ld%d" % (8 + 2 * hf), 2200.0)
         M = V("mx" + h)
-        scan(M, V("ps", 512 * bank, 512 * bank + H), V("cm"), -1.0e29, ALU.max, ALU.min)
+        scan(M, V("ps", 512 * bank, 512 * bank + H), V("cm"), -1.0e29, ALU.max, ALU.add)
         top, cnt = C("sm" + h, 96), C("sm" + h, 100)
         op({"v": vc(5)}, [M], [top], lambda q, T, e: q.tensor_reduce(ap(T, top), ap(T, (M[0], 31, H, 32)), AxisListType.X, ALU.max))
         op({"s": par["act"] + 20 + H * cy}, [M, top], [V("junk" + h), cnt],
            lambda q, T, e: q.activation(ap(T, V("junk" + h)), ap(T, M), ACT.Sign, bias=ap(T, top), scale=-1.0, accum_out=ap(T, cnt)))
         lr = lambda a, b: V("lr" + h, a, b)
         ts(lr(0, 4), V("cf", 20, 24), cnt, ALU.add)
-        ts(lr(4, 20), V("wa" + h), C("cf", 12), ALU.subtract, idx=lr(0, 1))
+        ts(lr(4, 20), V("wa" + h), C("cf", 32 + ADMAS[hf]), ALU.mult, -1.0, ALU.add, idx=lr(0, 1))
         rank = V("ka" + h, 0, 10)
-        tt(V("ka" + h, 0, 16), V("wk" + h, 0, 2 * W1), c2, ALU.add, idx=lr(0, 1))
-        tt(V("l2" + h, 0, 10), rank, V("kb" + h, 0, 10), ALU.max)
-        cp(lr(20, 30), V("l2" + h, 0, 10))
+        if t == 0 and hf in MARK0:
+            lin(V("mk" + h, 0, H), V("w0", 0, W1), idx=lr(4, 14))
+            scan(V("mk" + h, H, 2 * H), V("keep"), V("mk" + h, 0, H), 0.0, ALU.mult, ALU.add)
+            cp(V("si" + h, 0, 5), V("mk" + h, H + 31, 2 * H, 32))
+            ts(V("si" + h, 16, 26, 2), V("si" + h, 0, 5), 6, ALU.arith_shift_right, 511, ALU.bitwise_and)
+            ts(V("si" + h, 17, 26, 2), V("si" + h, 0, 5), 15, ALU.arith_shift_right)
+            tt(rank, V("si" + h, 16, 26), V("kb" + h, 0, 10), ALU.max)
+        else:
+            tt(V("ka" + h, 0, 16), V("wk" + h, 0, 2 * W1), V("kb" + h, 0, 16), ALU.max, idx=lr(0, 1))
+        ts(lr(20, 30), rank, 32.0, ALU.subtract)
         for b in range(4):
             lin(V("xh" + h, 336 * b + W1, 336 * b + 336), V("xh" + h, 336 * b, 336 * b + W1), idx=lr(4, 14))
-            tt((Z[0], b, 640, 4), V("xh" + h, 336 * b, 336 * b + 336), V("xi" + h, H * b, H * b + H), ALU.add, idx=lr(20, 30))
+            tt((Z[0], b, 640, 4), V("xh" + h, 336 * b, 336 * b + 336), V("xh" + h, 336 * b, 336 * b + H) if SAME else V("xi" + h, H * b, H * b + H), ALU.add, idx=lr(20, 30))
             lin((Z32[0], H * b, H * b + H, 1), (Z[0], b, 640, 4), 32.0)
         if t == 2:
-            lin(V("pw" + h, 0, W1), V("nat"), 1.0, float(H * hf))
+            iota(V("pw" + h, 0, W1), [[1, W1]], H * hf)
             lin(V("pw" + h, W1, W1 + H), V("pw" + h, 0, W1), idx=lr(4, 14))
             lin(V("fob", H * hf, H * hf + H), V("pw" + h), idx=lr(20, 30))
         quant(V("zq" + h), V("zs" + h), Z)
@@ -361,15 +440,15 @@ def build(par):
             tt(V("win" + h, 256 * b, 256 * b + H), V("ps", 512 * (bank + b), 512 * (bank + b) + H), (Z32[0], H * b, H * b + H, 1), ALU.add)
             lin(V("pt", base + b, base + 320, 4), V("win" + h, 256 * b, 256 * b + W1), 1.0 / 32, idx=lr(14, 19))
         quant(V("pq", 128 * k, 128 * k + 128), V("psc", 128 * k, 128 * k + 128), V("pt", base - 192, base + 320))
-        a, la = 128 * k + 48, 368 * hf + 128 + 80 * t
+        a, la = 128 * k + 48, 288 * hf + 48 + 80 * t
         op({"g": par["iss"]}, [V("pq", a, a + 80), V("psc", a, a + 80)], [V("landq", la, la + 80), V("lands", la, la + 80)], None,
-           kind="rem", sem="arr%d" % k, lat=par["rem"], step=STEP[t], a=a, la=la)
+           kind="rem", sem="arr%d" % k, lat=par["rem"] + (par["first"] if k == 0 else 0.0), step=STEP[t], moves=[("pq", a, "landq", la, 80), ("psc", a, "lands", la, 80)])
         lin(V("p16" + h), V("pt", base, base + 320), 16.0)
         if t == 0:
             depth(hf)
         tt(V("sa" + h, 2, 98, 3), V("wk" + h), V("ck" + h), ALU.add, idx=lr(2, 4))
         lin(V("sa" + h, 1, 30, 3), V("sa" + h, 50, 80, 3), -1024.0, 16384.0)
-        lin(V("sc" + h, 0, 30, 3), rank, 1024.0, -1024.0 * (W1 - 1))
+        lin(V("sc" + h, 0, 30, 3), rank, 1024.0, -1024.0 * (W1 + 31))
         scan(V("sm" + h, 128, 158), V("sa" + h, 0, 30), V("sc" + h, 0, 30), 0.0, ALU.min, ALU.max)
         cp(lr(70, 80), V("sm" + h, 130, 158, 3))
 
@@ -377,7 +456,7 @@ def build(par):
         h = "_%d" % hf
         now[0] = hf
         bank = 4 * hf
-        la = 368 * hf + 128 + 80 * t
+        la = 288 * hf + 48 + 80 * t
         for b in range(4):
             mm(bank + b, 128, V("eq", 128 * b, 128 * b + 128), V("es", 128 * b, 128 * b + 128), V("landq", la - 48, la + 80), V("lands", la - 48, la + 80))
         for b in range(4):
@@ -414,7 +493,7 @@ def depend(ops):
     writer = {n: np.full(s[1][1], -1) for n, s in SCRATCH.items()}
     readers = {n: [] for n in SCRATCH}
     for i, o in enumerate(ops):
-        dep = set()
+        dep = set(o.get("after", []))
         rd = [a for a in o["rd"] if a[0] != "ps"]
         wr = [a if a[0] != "ps" else ("ps", a[1] // 512 * 512, a[1] // 512 * 512 + 512, 1) for a in o["wr"] + [a for a in o["rd"] if a[0] == "ps"]]
         for a in rd + wr:
@@ -431,64 +510,90 @@ def depend(ops):
         o["dep"] = sorted(dep)
 
 
-def place(ops, seq, par, pre, eng, bias, back=False):
-    hop, xhop = par["hop"], par["xhop"]
-    line = {e: [] for e in "vspgy"}
-    start, done, out = {}, {}, {}
+def place(ops, seq, par, pre, eng, bias, back=False, tail=False):
+    hop = par["hop"]
+    lo, hi = {e: [] for e in "vspgy"}, {e: [] for e in "vspgy"}
+    n = len(ops)
+    start, done, out = [0.0] * n, [0.0] * n, [None] * n
     for i in seq:
-        o, best = ops[i], None
-        for e, d in o["dur"].items():
-            if eng[i] is not None and eng[i] != e:
-                continue
-            st = 0.0
-            for j in pre[i]:
-                x = done[j] + (hop if out[j] == e else xhop)
-                if x > st:
-                    st = x
-            if back:
-                st += o.get("lat", 0.0)
-            ln = line[e]
-            k = len(ln)
-            while k > 0 and ln[k - 1][1] > st:
+        ready = 0.0
+        for j in pre[i]:
+            if done[j] > ready:
+                ready = done[j]
+        if pre[i]:
+            ready += hop
+        dur, lat = ops[i]
+        best = None
+        for e in (dur if eng[i] is None else eng[i]):
+            d = dur[e]
+            st = ready + lat[e] if back else ready
+            a, b = lo[e], hi[e]
+            k = m = len(a)
+            if tail and m:
+                st = max(st, b[-1])
+            while k > 0 and b[k - 1] > st:
                 k -= 1
-            while k < len(ln) and ln[k][0] < st + d:
-                st = max(st, ln[k][1])
+            while k < m and a[k] < st + d:
+                if b[k] > st:
+                    st = b[k]
                 k += 1
-            key = st + d * (bias if e == "v" else 1.0)
+            key = st + d * (bias if e == "v" else 1.0) + (0.0 if back else lat[e])
             if best is None or key < best[0]:
                 best = (key, st, e, d, k)
         key, st, e, d, k = best
-        line[e].insert(k, (st, st + d))
-        start[i], done[i], out[i] = st, st + d + (0.0 if back else o.get("lat", 0.0)), e
+        lo[e].insert(k, st)
+        hi[e].insert(k, st + d)
+        start[i], done[i], out[i] = st, st + d + (0.0 if back else lat[e]), e
     return start, done, out
 
 
-def replay(ops, order, eng, par):
-    free = dict.fromkeys("vspgy", 0.0)
-    done = {}
+def replay(ops, order, eng, par, pre, chain=False):
+    hop = par["hop"]
+    free, last = dict.fromkeys("vspgy", 0.0), dict.fromkeys("vspgy", -1)
+    n = len(ops)
+    done, why = [0.0] * n, [-1] * n
     for i in order:
         e = eng[i]
-        st = free[e]
-        for j in ops[i]["dep"]:
-            x = done[j] + (par["hop"] if eng[j] == e else par["xhop"])
-            if x > st:
-                st = x
-        free[e] = st + ops[i]["dur"][e]
-        done[i] = free[e] + ops[i].get("lat", 0.0)
-    return max(done.values())
+        st, w = free[e] - hop, last[e]
+        for j in pre[i]:
+            if done[j] > st:
+                st, w = done[j], j
+        dur, lat = ops[i]
+        free[e] = st + hop + dur[e]
+        done[i], why[i], last[e] = free[e] + lat[e], w, i
+    end = max(done)
+    if not chain:
+        return end
+    i, pairs = done.index(end), []
+    while why[i] >= 0:
+        if why[i] not in pre[i]:
+            pairs.append((why[i], i))
+        i = why[i]
+    return end, pairs
 
 
 def arrange(ops, par, others, tries):
     n = len(ops)
-    pre = [o["dep"] for o in ops]
+    pre, anc = [], []
+    for o in ops:
+        a = 0
+        for j in o["dep"]:
+            a |= anc[j]
+        pre.append([j for j in o["dep"] if not a >> j & 1])
+        for j in o["dep"]:
+            a |= 1 << j
+        anc.append(a)
     succ = [[] for _ in ops]
     for i in range(n):
         for j in pre[i]:
             succ[j].append(i)
+    half = [o["hf"] for o in ops]
+    others = [([(o["dur"], o["lat"]) for o in q], p) for q, p in others]
+    ops = others[0][0]
     tail = [0.0] * n
     for i in range(n - 1, -1, -1):
-        tail[i] = min(ops[i]["dur"].values()) + ops[i].get("lat", 0.0) + max([tail[j] + par["hop"] for j in succ[i]] + [0.0])
-    x = [12345]
+        tail[i] = min(ops[i][0][e] + ops[i][1][e] for e in ops[i][0]) + max([tail[j] + par["hop"] for j in succ[i]] + [0.0])
+    x = [SEED]
 
     def rnd():
         x[0] = (x[0] * 1103515245 + 12345) % 2147483648
@@ -500,40 +605,92 @@ def arrange(ops, par, others, tries):
             for j in succ[i]:
                 if pr[i] >= pr[j]:
                     pr[i] = pr[j] - 1e-3
-        return sorted(range(n), key=lambda i: (pr[i], i))
-    flex = [i for i in range(n) if len(ops[i]["dur"]) > 1]
+        return [i for _, i in sorted(zip(pr, range(n)))]
+    flex = [i for i in range(n) if len(ops[i][0]) > 1]
     best, top = None, None
     for it in range(tries):
         if it < 40:
-            pr = [-tail[i] + 1000.0 * (it % 10) * ops[i]["hf"] for i in range(n)]
+            pr = [-tail[i] + 1000.0 * (it % 10) * half[i] for i in range(n)]
             bias, fix = 1.0 + 0.7 * (it // 10), [None] * n
         else:
             pr, fix, bias = list(best[3]), list(best[2]), 1.0
             a, w = rnd() * best[4], 300 + 3000 * rnd() * rnd()
             u = rnd()
-            if u < 0.35:
+            if u < MIX[0] and best[6]:
+                i, j = best[6][int(rnd() * len(best[6]))]
+                v = rnd()
+                k = i if rnd() < 0.5 else j
+                if v < 0.4 and len(ops[k][0]) > 1:
+                    alt = [e for e in ops[k][0] if e != fix[k]]
+                    fix[k] = alt[int(rnd() * len(alt))]
+                elif v < 0.7:
+                    pr[j] = pr[i] - 1.0 - 600.0 * rnd() * rnd()
+                else:
+                    pr[i] = pr[j] + 1.0 + 600.0 * rnd() * rnd()
+            elif u < MIX[1]:
                 amp = 100 + 1500 * rnd()
                 pr = [s + (amp * (rnd() - 0.5) if a < s < a + w else 0.0) for s in pr]
-            elif u < 0.6:
+            elif u < MIX[2]:
                 amp, hf = 2000 * (rnd() - 0.5), int(rnd() * 2)
-                pr = [s + (amp if a < s < a + w and ops[i]["hf"] == hf else 0.0) for i, s in enumerate(pr)]
+                pr = [s + (amp if a < s < a + w and half[i] == hf else 0.0) for i, s in enumerate(pr)]
             else:
                 for _ in range(1 + int(rnd() * 2)):
                     i = flex[int(rnd() * len(flex))]
-                    alt = [e for e in ops[i]["dur"] if e != fix[i]]
+                    alt = [e for e in ops[i][0] if e != fix[i]]
                     fix[i] = alt[int(rnd() * len(alt))]
         start, done, eng = place(ops, legal(pr), par, pre, fix, bias)
         if it < 40 or it % JUST == 0:
-            fix = [eng[i] for i in range(n)]
-            s2, d2, e2 = place(ops, legal([start[i] + ops[i]["dur"][eng[i]] for i in range(n)])[::-1], par, succ, fix, 1.0, True)
-            start, done, eng = place(ops, legal([-d2[i] for i in range(n)]), par, pre, fix, 1.0)
-        order = sorted(range(n), key=lambda i: (start[i], i))
-        cost = sum(replay(q, order, eng, p) for q, p in others) / len(others)
-        if best is None or cost <= best[0] + (0.0 if it < 40 else TEMP * (1.0 - it / tries)):
-            best = (cost, order, [eng[i] for i in range(n)], [start[i] for i in range(n)], max(done.values()), [done[i] for i in range(n)])
+            s2, d2, e2 = place(ops, legal([start[i] + ops[i][0][eng[i]] for i in range(n)])[::-1], par, succ, eng, 1.0, True)
+            start, done, eng = place(ops, legal([-d for d in d2]), par, pre, eng, 1.0)
+        order = [i for _, i in sorted(zip(start, range(n)))]
+        cost = sum(replay(q, order, eng, p, pre) for q, p in others) / len(others)
+        if best is None or cost <= best[0] + (0.0 if it < 40 else TEMP * (1.0 - it / tries) * rnd() * 2.0):
+            q, p = others[it % len(others)]
+            best = (cost, order, eng, start, max(done), done, replay(q, order, eng, p, pre, True)[1])
             if top is None or cost < top[0]:
                 top = best
-    return top[1], top[2], top[5], top[0]
+    cost, order, eng = top[0], list(top[1]), list(top[2])
+    keep = (cost, order, eng)
+    pairs = top[6]
+    for at in range(MOVES * AGAIN):
+        it = at % MOVES
+        if at and not it:
+            cost, order, eng = keep
+            pairs = replay(ops, order, eng, par, pre, True)[1]
+        if not pairs:
+            break
+        i, j = pairs[int(rnd() * len(pairs))]
+        u = rnd()
+        o2, e2 = order, eng
+        if u < 0.25:
+            k = i if rnd() < 0.5 else j
+            if len(ops[k][0]) < 2:
+                continue
+            alt = [e for e in ops[k][0] if e != eng[k]]
+            e2 = list(eng)
+            e2[k] = alt[int(rnd() * len(alt))]
+        else:
+            a, b = order.index(i), order.index(j)
+            far = int(12 * rnd() * rnd() * rnd())
+            if u < 0.6:
+                a = max(0, a - far)
+                m = anc[j] | 1 << j
+                mid = order[a:b + 1]
+                o2 = order[:a] + [k for k in mid if m >> k & 1] + [k for k in mid if not m >> k & 1] + order[b + 1:]
+            else:
+                b = min(n - 1, b + far)
+                mid = order[a:b + 1]
+                o2 = order[:a] + [k for k in mid if k != i and not anc[k] >> i & 1] + [k for k in mid if k == i or anc[k] >> i & 1] + order[b + 1:]
+        c = sum(replay(q, o2, e2, p, pre) for q, p in others) / len(others)
+        if c <= cost + TEMP2 * (1.0 - it / MOVES) * rnd() * rnd():
+            cost, order, eng = c, o2, e2
+            q, p = others[it % len(others)]
+            pairs = replay(q, order, eng, p, pre, True)[1]
+            if cost < keep[0]:
+                keep = (cost, order, eng)
+    cost, order, eng = keep
+    start, done, out = place(ops, order, par, pre, eng, 1.0, False, True)
+    return order, eng, done, cost
 
 
 def plan(tries):
@@ -569,11 +726,11 @@ def rank_program(g, core, T, topo):
                 for s2, c2 in known[j].items():
                     seen[e][s2] = max(seen[e].get(s2, 0), c2)
         known[i] = dict(seen[e])
-        if o["kind"] == "c":
+        if o["kind"] == "c" and e != "y":
             o["emit"](q, T, e).then_inc(T.sem[e], 1)
             count[e] += 1
             mark[i] = (e, count[e])
-        elif o["kind"] == "dma":
+        elif o["kind"] != "rem":
             o["emit"](q, T, e).then_inc(T.sem[o["sem"]], 16)
             count[o["sem"]] = count.get(o["sem"], 0) + 16
             mark[i] = (o["sem"], count[o["sem"]])
@@ -581,9 +738,9 @@ def rank_program(g, core, T, topo):
             peer = T.cores[rank ^ o["step"]]
             rid, pid = topo.addr(peer, core)
             m, n = topo.mask(core, peer), len(topo.engines(core, peer))
-            a, la = o["a"], o["la"]
-            g.remote_dma(T.landq[:, la:la + 80].bitcast(dt.uint8), T.pq[:, a:a + 80].bitcast(dt.uint8), T.sem[o["sem"]], T.sem.sent, pid, rid, m)
-            g.remote_dma(T.lands[:, la:la + 80], T.psc[:, a:a + 80], T.sem[o["sem"]], T.sem.sent, pid, rid, m)
+            a, la, w = o["moves"][0][1], o["moves"][0][3], o["moves"][0][4]
+            g.remote_dma(T.landq[:, la:la + w].bitcast(dt.uint8), T.pq[:, a:a + w].bitcast(dt.uint8), T.sem[o["sem"]], T.sem.sent, pid, rid, m)
+            g.remote_dma(T.lands[:, la:la + w], T.psc[:, a:a + w], T.sem[o["sem"]], T.sem.sent, pid, rid, m)
             count["sent"] += 2 * n
             mark[i] = (o["sem"], 2 * n)
             known[i] = {}

import numpy as np
from concourse.mybir import dt, AluOpType as ALU, AxisListType, ActivationFunctionType as ACT

H = 160
W1 = 176
END = 168
STEP = [1, 2, 4]
BF, F32, I32, U16, CODE, U8 = "bfloat16", "float32", "int32", "uint16", "float8_e4m3fn_x4", "uint8"

SCRATCH = {}
for _n, _w, _d in [
        ("fnb", 20, I32), ("ub", 512, BF), ("vb", 512, BF), ("uq", 128, CODE), ("us", 128, U8), ("uq2", 128, CODE), ("us2", 128, U8),
        ("vq", 128, CODE), ("vs", 128, U8), ("wq", 512, CODE), ("wsc", 512, U8), ("eb", 2048, BF), ("e16", 128, BF), ("e0", 516, BF), ("eq", 512, CODE), ("es", 512, U8),
        ("landq", 576, CODE), ("lands", 576, U8), ("pq", 768, CODE), ("psc", 768, U8), ("pt", 8 * 288, BF),
        ("ci", 64, I32), ("cf", 64, F32), ("nat", W1 + 2, BF), ("natn", H, BF), ("tm16", H, BF), ("xl", H, BF), ("xb", H, BF),
        ("cv", H, BF), ("wt", H, BF), ("w0", 2 * W1, F32), ("a0", W1, BF), ("ta", 32, F32),
        ("keep", H, BF), ("w1", H, F32), ("cm", H, BF), ("s32", 320, F32), ("cw", 80, F32), ("cu", 32, U16), ("fob", 320, F32), ("yb", 320, F32)]:
    SCRATCH[_n] = ("sbuf", [128, _w], _d)
for _h in "01":
    for _n, _w, _d in [
            ("x", 640, BF), ("xh", 4 * 336, BF), ("ka", 40, F32), ("kb", 24, F32), ("z", 640, BF), ("xi", 640, BF), ("z32", 640, BF), ("win", 1024, BF), ("p16", 320, BF),
            ("xq", H, CODE), ("xs", H, U8), ("zq", H, CODE), ("zs", H, U8),
            ("fr", 12 * W1, BF), ("tb", 12 * H, BF), ("ls", 16 * 12, U16), ("sa", 112, F32), ("sc", 32, F32), ("av", W1, BF), ("nx", W1, BF), ("tc", 64, F32),
            ("up", W1 + H, BF), ("pw", W1 + H, F32), ("ur", 6 * W1, BF), ("wr", 12 * W1, F32), ("wi", W1, I32), ("ar", 10 * W1, BF), ("wa", 2 * W1, BF),
            ("wk", 3 * W1, I32), ("mk", 2 * H, F32), ("si", 32, I32), ("sm", 256, F32), ("ck", 32, F32), ("mx", H, F32), ("junk", H, BF), ("lr", 96, U16)]:
        SCRATCH[_n + "_" + _h] = ("sbuf", [128, _w], _d)
SCRATCH["ps"] = ("psum", [128, 4096], F32)

SEMAPHORES = ["v", "s", "p", "g", "sent", "out"] + ["ld%d" % k for k in range(15)] + ["arr%d" % k for k in range(6)]
SEMAPHORES += ["cp%d" % k for k in range(8)] + ["sel%d" % k for k in range(6)] + ["cw"] + ["dw%d" % k for k in range(8)]
ADMAS = (4, 4)
MARK0 = (1,)
FRADIX, FSTEPS = [4, 3], [1, 1, 2, 2]
SAME = False
XDMA = True
RADIX = [4, 4]

PAR = {"cy": 1.04, "g": 1.3, "sc": 3.2, "hop": 175.0, "xhop": 175.0, "load": 2500.0, "rem": 3300.0, "act": 65.0, "iss": 300.0, "fx": 0.0, "dq": 100.0, "loc": 1900.0, "first": 1500.0}
SETS = [{}, {"cy": 0.85, "g": 1.0, "sc": 1.8, "hop": 190.0, "first": 800.0, "loc": 2200.0},
        {"cy": 1.2, "g": 1.7, "sc": 4.5, "hop": 200.0, "rem": 4500.0, "iss": 600.0, "first": 2500.0},
        {"g": 1.6, "load": 1700.0, "rem": 2600.0, "loc": 1400.0, "first": 1500.0}]
TRIES = 4000
MOVES, TEMP2 = 22000, 60.0
AGAIN = 3
JUST, TEMP, SEED, MIX = 1, 100.0, 1, (0.5, 0.65, 0.8)


def size(a):
    return len(range(a[1], a[2], a[3]))


def two(*vs):
    return all(SCRATCH[a[0]][2] in (BF, U16) for a in vs)


def V(buf, a=0, b=None, s=1):
    return (buf, a, SCRATCH[buf][1][1] if b is None else b, s)


def C(buf, k):
    return (buf, k, k + 1, 1)


def ap(T, a):
    if isinstance(a, tuple):
        return T[a[0]][:, a[1]:a[2]] if a[3] == 1 else T[a[0]][:, a[1]:a[2]:a[3]]
    return a


def views(*xs):
    return [a for a in xs if isinstance(a, tuple)]


def build(par):
    ops, now = [], [0]
    cy, ga = par["cy"], par["g"]

    def op(dur, rd, wr, emit, kind="c", lat=0.0, **kw):
        lat = {e: (lat.get(e, 0.0) if isinstance(lat, dict) else lat) for e in dur}
        ops.append(dict(hf=now[0], dur=dur, lat=lat, rd=views(*rd), wr=views(*wr), emit=emit, kind=kind, **kw))

    def vc(n):
        return max(n * cy + par["fx"], 64 * cy)

    def ts(out, a, s1, op0, s2=None, op1=None, idx=None):
        def emit(q, T, e):
            x = ap(T, a) if idx is None else ap(T, a).indirect(ap(T, idx))
            if op1 is None:
                return q.tensor_scalar(ap(T, out), x, ap(T, s1), None, op0)
            return q.tensor_scalar(ap(T, out), x, ap(T, s1), ap(T, s2), op0, op1)
        d = vc(size(out) * (0.5 if two(out, a) else 1)) if idx is None else 50 + ga * size(out)
        op({"v": d}, [a, s1, s2, idx], [out], emit)

    def tt(out, a, b, o, idx=None):
        def emit(q, T, e):
            x = ap(T, a) if idx is None else ap(T, a).indirect(ap(T, idx))
            return q.tensor_tensor(ap(T, out), x, ap(T, b), o)
        d = vc(size(out) * (1 if a[0] == "ps" else 2)) if idx is None else 50 + ga * size(out)
        op({"v": d}, [a, b, idx], [out], emit)

    def cp(out, a):
        op({"v": vc(size(out))}, [a], [out], lambda q, T, e: q.tensor_copy(ap(T, out), ap(T, a)))

    def lin(out, a, scale=1.0, bias=0.0, idx=None, eng="vs"):
        def emit(q, T, e):
            x = ap(T, a) if idx is None else ap(T, a).indirect(ap(T, idx))
            if e == "s":
                if isinstance(bias, float) and bias == 0.0:
                    if isinstance(scale, tuple):
                        return q.activation(ap(T, out), x, ACT.Identity, scale=ap(T, scale))
                    return q.activation(ap(T, out), x, ACT.Copy, scale=scale) if scale != 1.0 else q.activation(ap(T, out), x, ACT.Copy)
                return q.activation(ap(T, out), x, ACT.Identity, bias=ap(T, bias), scale=ap(T, scale))
            if isinstance(bias, float) and bias == 0.0:
                return q.tensor_scalar(ap(T, out), x, ap(T, scale), None, ALU.mult) if scale != 1.0 else q.tensor_copy(ap(T, out), x)
            return q.tensor_scalar(ap(T, out), x, ap(T, scale), ap(T, bias), ALU.mult, ALU.add)
        n = size(out)
        if idx is None:
            d = {"v": vc(n * (0.5 if two(out, a) else 1)), "s": par["act"] + n * cy}
        else:
            d = {"v": 50 + ga * n, "s": 65 + ga * n}
        op({e: d[e] for e in eng}, [a, scale, bias, idx], [out], emit)

    def dup(out, a, sem=None):
        n = size(out)

        def emit(q, T, e):
            if e == "y":
                return q.dma_start(ap(T, out), ap(T, a))
            if e == "g":
                return q.affine_select(ap(T, out), ap(T, a), [[0, n]], ALU.is_equal, 0.0, 0, 0)
            return q.tensor_copy(ap(T, out), ap(T, a)) if e == "v" else q.activation(ap(T, out), ap(T, a), ACT.Copy)
        d = {"v": vc(n * (0.5 if two(out, a) else 1)), "s": par["act"] + n * cy, "g": 170 + 2 * cy * n}
        if sem:
            d["y"] = par["dq"]
        op(d, [a], [out], emit, lat={"y": par["loc"]}, sem=sem)

    def scan(out, d0, d1, init, op0, op1):
        op({"v": vc(size(out) * (0.5 if two(out, d0, d1) else 1))}, [d0, d1], [out],
           lambda q, T, e: q.tensor_tensor_scan(ap(T, out), ap(T, d0), ap(T, d1), init, op0, op1))

    def fill(out, c, eng="vg"):
        d = {"v": vc(size(out) * (0.5 if two(out) else 1))}
        if SCRATCH[out[0]][2] != U16:
            d["g"] = 130 + 2 * cy * size(out)
        d = {e: d[e] for e in eng if e in d}
        op(d, [], [out], lambda q, T, e: q.memset(ap(T, out), c) if e == "v" else
           (q.iota(ap(T, out), [[0, size(out)]], int(c), 0) if SCRATCH[out[0]][2] == I32 else q.iota(ap(T, out), [[0, size(out)]], int(c), 0, allow_small_or_imprecise_dtypes=True)))

    def iota(out, pat, base, cm=0):
        def emit(q, T, e):
            if SCRATCH[out[0]][2] == I32:
                return q.iota(ap(T, out), pat, base, cm)
            return q.iota(ap(T, out), pat, base, cm, allow_small_or_imprecise_dtypes=True)
        op({"g": 130 + 2 * cy * size(out)}, [], [out], emit)

    def select(out, a, pat, base, cm, fillv):
        op({"g": 170 + 2 * cy * size(out)}, [a], [out], lambda q, T, e: q.affine_select(ap(T, out), ap(T, a), pat, ALU.is_equal, fillv, base, cm))

    def quant(q_, s_, a):
        op({"v": 12 + 0.22 * size(a)}, [a], [q_, s_], lambda q, T, e: q.quantize_mx(ap(T, q_), ap(T, s_), ap(T, a)))

    def mm(bank, n, lq, lsc, rq, rsc):
        out = V("ps", 512 * bank, 512 * bank + n)
        op({"p": (n + 16) * 1.1}, [lq, lsc, rq, rsc], [out], lambda q, T, e: q.matmul_mx(ap(T, out), ap(T, lq), ap(T, lsc), ap(T, rq), ap(T, rsc), True, True))

    def dma(eng, rd, wr, f, sem, lat):
        op({e: par["dq"] for e in eng}, rd, wr, lambda q, T, e: q.dma_start(*f(T)), kind="dma", sem=sem, lat=lat)

    def wrap(lst, rep, tmp):
        scan(tmp, rep, V("cv"), 1.0, ALU.min, ALU.subtract)
        ts(lst, (tmp[0], tmp[1] + 15, tmp[2], 16), -1.0, ALU.mult, 255.0, ALU.add)

    L = par["load"]
    dma("y", [], [V("fnb")], lambda T: (T.fnb[:], T.fn[:]), "ld0", L - 300)
    dma("s", [], [V("ub")], lambda T: (T.ub[:], T.u[:]), "ld1", L)
    dma("y", [], [V("x_0")], lambda T: (T.x_0[:], T.x[:, 0:640]), "ld2", L + 200)
    dma("y", [], [V("x_1")], lambda T: (T.x_1[:], T.x[:, 640:1280]), "ld3", L + 600)
    dma("y", [], [V("wq")], lambda T: (T.wq[:].bitcast(dt.uint8), T.wc[:]), "ld4", L + 1500)
    dma("y", [], [V("wsc")], lambda T: (T.wsc[:], T.ws[:]), "ld5", L + 1500)
    dma("y", [], [V("vb")], lambda T: (T.vb[:], T.v[:]), "ld6", L + 2000)

    ri, rf, r16 = C("ci", 1), C("cf", 0), C("cf", 1)
    iota(C("ci", 0), [[0, 1]], 0, 1)
    iota(V("nat"), [[1, W1 + 2]], 0)
    iota(V("tm16"), [[0, 10], [512, 16]], 0)
    ts(ri, C("ci", 0), 15, ALU.bitwise_and)
    cp(rf, ri)
    lin(r16, rf, 1.0, 16.0)
    lin(C("cf", 2), rf, -512.0, 256.0)
    lin(C("cf", 3), rf, -16.0, 240.0)
    ts(C("cf", 4), C("cf", 3), C("cf", 3), ALU.mult, 256.0, ALU.add)
    lin(V("cv"), V("tm16"), 1.0, C("cf", 2))
    ts(V("cv", 15, H, 16), V("tm16", 0, H, 16), C("cf", 4), ALU.subtract)
    iota(V("natn"), [[-1, H]], -1)
    iota(V("xl"), [[0, 5], [1, 32]], 0)
    ts(C("cf", 5), rf, 0.0, ALU.not_equal)
    ts(C("cf", 6), C("cf", 5), float(END), ALU.add)
    iota(V("cw", 0, 10), [[0, 5], [16, 2]], 0)
    ts(V("cu", 0, 10), V("cw", 0, 10), rf, ALU.add)
    nat32 = V("nat", 0, 32)
    ts(V("s32", 0, 32), nat32, r16, ALU.is_equal)
    ts(V("s32", 32, 64), nat32, rf, ALU.is_equal)
    tt(V("s32", 64, 96), V("s32", 0, 32), V("s32", 32, 64), ALU.subtract)
    tt(V("wt"), V("s32", 64, 96), V("nat", END + 1, END + 1 - H, -1), ALU.mult, idx=V("cu", 0, 10))
    ts(V("keep"), V("xl"), 1.0, ALU.min)
    iota(V("cw", 16, 26), [[16, 10]], 0)
    iw = V("cw", 32, 42)
    lin(iw, V("cw", 16, 26), 1.0, rf)
    fill(V("ta", 0, 20), -1.0e6)
    lin(V("ta", 1, 20, 2), iw, 1.0, float(W1))
    iota(V("xb"), [[32, 5], [0, 32]], W1 + 32)
    ts(V("s32", 96, 128), nat32, rf, ALU.is_lt, 64.0, ALU.mult)
    ts(V("s32", 160, 192), nat32, r16, ALU.is_lt, 32768.0, ALU.mult)
    lin(V("s32", 128, 160), V("s32", 32, 64), 64.0)
    lin(V("s32", 192, 224), V("s32", 0, 32), 32768.0)
    tt(V("s32", 224, 288), V("s32", 96, 160), V("s32", 160, 224), ALU.add)
    lin(V("s32", 288, 320), V("s32", 224, 256), 1.0, 1.0)
    tt(V("w1"), V("s32", 256, 288), V("xb"), ALU.mult, idx=V("cu", 0, 10))
    tt(V("w0", 0, H), V("s32", 288, 320), V("w1"), ALU.add, idx=V("cu", 0, 10))
    fill(V("w0", H, W1), 0.0)
    dup(V("w0", W1, 2 * W1), V("w0", 0, W1), "cw")
    k0 = min(ADMAS) // 2
    for k in sorted({0} | set(range(k0, 4))):
        ts(C("ci", 2 + k), ri, 1 << k, ALU.bitwise_and)
    ts(V("cf", 8 + k0, 12), V("ci", 2 + k0, 6), 0.0, ALU.is_gt, 256.0, ALU.mult)
    fill(C("cf", 28), -1.0)
    ts(V("cf", 24 + k0, 28), V("cf", 8 + k0, 12), -255.0 / 65536, ALU.mult, 1.0, ALU.add)
    for k in set(ADMAS):
        op({"v": vc(4)}, [V("cf", 24 + k // 2, 29)], [C("cf", 32 + k)], lambda q, T, e, k=k: q.tensor_reduce(T.cf[:, 32 + k:33 + k], T.cf[:, 24 + k // 2:29], AxisListType.X, ALU.mult))
    ts(C("ci", 6), ri, 1, ALU.arith_shift_right)
    ts(C("cf", 13), ri, 10.0, ALU.is_ge, -8.0, ALU.mult)
    ts(C("cf", 14), ri, -10.0, ALU.add, 4.0, ALU.min)
    blk = C("cf", 15)
    ts(blk, C("ci", 6), C("cf", 13), ALU.add, C("cf", 14), ALU.max)
    ts(C("cf", 16), ri, 10.0, ALU.is_lt, float(W1), ALU.mult)
    ts(C("cf", 17), C("ci", 2), C("cf", 16), ALU.mult, -2.0 * W1, ALU.add)
    lin(C("cf", 18), blk, 32.0, 2.0 * W1 - 128)
    lin(V("cf", 22, 24), V("nat", 0, 2), 0.0, C("cf", 18))
    lin(V("cf", 20, 22), V("cf", 22, 24), 1.0, C("cf", 17))
    lin(C("cf", 19), blk, 32.0, float(W1 + 32))
    ts(V("cm"), V("xb"), C("cf", 19), ALU.not_equal, -2.0e29, ALU.mult)
    c3 = V("cw", 64, 74)
    iota(c3, [[16, 5], [0, 2]], W1 - 256)
    iota(V("ci", 16, 24), [[16, 8]], 0)
    cp(V("cu", 16, 24), V("ci", 16, 24))
    quant(V("uq"), V("us"), V("ub"))
    op({"v": 50 + ga * 128}, [V("uq"), V("cu", 16, 24)], [V("uq2")],
       lambda q, T, e: q.tensor_copy(T.uq2[:, 0:128].bitcast(dt.uint32), T.uq[:, 0:128].bitcast(dt.uint32).indirect(T.cu[:, 16:24])))
    op({"s": 65 + ga * 128}, [V("us"), V("cu", 16, 24)], [V("us2")],
       lambda q, T, e: q.activation(T.us2[:, 0:128], T.us[:, 0:128].indirect(T.cu[:, 16:24]), ACT.Copy))
    quant(V("vq"), V("vs"), V("vb"))
    iota(V("e16"), [[0, 128]], 16)
    iota(V("e0"), [[0, 516]], 0)
    select(V("e0", 3, 515, 4), V("e16"), [[-1, 128]], 0, 1, 0.0)
    for b in range(4):
        dma("y", [V("e0")], [V("eb", 512 * b, 512 * b + 512)], lambda T, b=b: (T.eb[:, 512 * b:512 * b + 512], T.e0[:, 3 - b:515 - b]), "ld%d" % (11 + b), 2500.0)
    quant(V("eq"), V("es"), V("eb"))
    for hf in range(2):
        fill(V("pt", 1152 * hf, 1152 * hf + 192), 0.0, "g")

    def tree(hf):
        h = "_%d" % hf
        now[0] = hf
        ls = lambda k, n=10: V("ls" + h, 12 * k, 12 * k + n)
        fr = lambda k: V("fr" + h, W1 * k, W1 * k + H)
        tb = lambda k: V("tb" + h, H * k, H * k + H)
        up = V("up" + h)
        fill(V("ls" + h, 12 * 7 + 10, 12 * 12, 12), END)
        for b in range(4):
            fill(V("win" + h, 256 * b + H, 256 * b + W1), 0.0, "g")
            fill(V("xh" + h, 336 * b + H, 336 * b + W1), 0.0, "g")
        fill(V("up" + h, H, W1 + H), -float(END + 1), "g")
        fill(C("up" + h, END + 1), 1.0, "g")
        fill(C("av" + h, H), -float(END + 1), "g")
        fill(V("kb" + h, 0, 16), 0.0, "g")
        ts(ls(0), V("fnb", 10 * hf, 10 * hf + 10), float(H * hf), ALU.subtract)
        ts(V("tc" + h, 1, 20, 2), V("fnb", 10 * hf, 10 * hf + 10), float(H * hf), ALU.subtract)
        lin(V("up" + h, 0, H), V("natn", 0, H), idx=ls(0))
        f, nf = V("up" + h, 0, H), 0
        for k, rx in enumerate(FRADIX):
            for j in range(rx - 1):
                lin(fr(nf), f, idx=ls(k))
                f = fr(nf)
                nf += 1
            wrap(ls(k + 1), f, tb(k))
        f = V("wt")
        for k in FSTEPS:
            lin(fr(nf), f, idx=ls(k))
            f = fr(nf)
            nf += 1
        scan(tb(4), V("keep"), f, 0.0, ALU.mult, ALU.min)
        scan(tb(5), V("keep"), f, 0.0, ALU.mult, ALU.max)
        lo, hi = (tb(4)[0], tb(4)[1] + 31, tb(4)[2], 32), (tb(5)[0], tb(5)[1] + 31, tb(5)[2], 32)
        cyc = ls(5)
        ts((cyc[0], cyc[1], cyc[2], 2), lo, C("cf", 5), ALU.mult, C("cf", 6), ALU.add)
        ts((cyc[0], cyc[1] + 1, cyc[2], 2), hi, -1.0, ALU.mult, float(END + 1), ALU.add)
        lin(V("av" + h, 0, H), V("up" + h, 0, W1), idx=cyc)
        back_ = V("av" + h, H, 0, -1)
        scan(V("nx" + h, W1 - 1, W1 - 1 - H, -1), back_, back_, 0.0, ALU.mult, ALU.min)
        ts(V("tc" + h, 0, 20, 4), lo, 0.0, ALU.is_equal, 1024.0, ALU.mult)
        ts(V("tc" + h, 2, 20, 4), hi, 0.0, ALU.is_equal, 1024.0, ALU.mult)
        scan(V("tc" + h, 32, 52), V("ta", 0, 20), V("tc" + h, 0, 20), 0.0, ALU.min, ALU.max)
        cp(ls(6), V("tc" + h, 33, 52, 2))
        nx = V("nx" + h, W1 - H, W1)
        op({"v": 50 + par["sc"] * H}, [nx, ls(6)], [up], lambda q, T, e: q.tensor_copy(ap(T, up).indirect(ap(T, ls(6))), ap(T, nx)))
        w = lambda name, k, n=W1: V(name + h, W1 * k, W1 * k + n)
        u, wsum, wdup, anc, pre = V("up" + h, 0, W1), V("w0", 0, W1), V("w0", W1, 2 * W1), w("ar", 0), w("ar", 1)
        nu, nw, na, bit, ADMA = 0, 0, 2, 0, ADMAS[hf]
        iota(anc, [[-1, W1]], -1)
        rows = []

        def pick(m, src):
            dma("y", [src, anc], [], lambda T: (T["ar" + h][m:128:4, 0:W1], T[src[0]][m:128:4, src[1]:src[2]]), "sel%d" % (3 * hf + m - 1), par["loc"])
            rows.append(len(ops) - 1)
        if ADMA:
            pick(1, u)
        else:
            lin(pre, anc, C("cf", 8))
        for k, rx in enumerate(RADIX + [0]):
            wrap(ls(7 + k), (u[0], u[1], u[1] + H, 1), tb(6 + k))
            lst = ls(7 + k, 11)
            if rx == 0:
                tt(w("wi", 0, H), wsum, wdup, ALU.add, idx=ls(7 + k))
                lin(w("wa", 1, H), anc, idx=ls(7 + k))
                break
            last = k == len(RADIX) - 1
            for j in range(rx - 1):
                short = last and j == rx - 2
                lin(w("ur", nu, H if short else W1), u, idx=ls(7 + k) if short else lst)
                u = w("ur", nu)
                nu += 1
                if k == 0 and j + 2 < ADMA:
                    pick(j + 2, u)
            tt(w("wr", nw), wsum, wdup, ALU.add, idx=lst)
            wsum = w("wr", nw)
            nw += 1
            if (2 << bit) > ADMA:
                a1 = w("wa", 0) if last and rx == 2 else w("ar", na)
                tt(a1, pre, anc, ALU.min, idx=lst)
                ops[-1]["after"] = list(rows)
                anc = a1
                na += 1
            bit += 1
            if rx == 4:
                lin(w("wr", nw), wsum, idx=lst)
                tt(w("wr", nw + 1), w("wr", nw), wsum, ALU.add, idx=lst)
                wsum = w("wr", nw + 1)
                nw += 2
                if (2 << bit) > ADMA:
                    lin(w("ar", na), anc, C("cf", 8 + bit), idx=lst)
                    ops[-1]["after"] = list(rows)
                    a1 = w("wa", 0) if last else w("ar", na + 1)
                    tt(a1, w("ar", na), anc, ALU.min, idx=lst)
                    anc = a1
                    na += 2
                bit += 1
            if last:
                wdup = w("wr", nw, H)
                dup(wdup, (wsum[0], wsum[1], wsum[1] + H, 1), "dw%d" % (4 * hf + k))
            else:
                wdup = w("wr", nw)
                nw += 1
                dup(wdup, wsum, "dw%d" % (4 * hf + k))
                pre = w("ar", na)
                na += 1
                lin(pre, anc, C("cf", 8 + bit))
                ops[-1]["after"] = list(rows)
        wsum = w("wi", 0, H)
        ts(w("wk", 1, H), wsum, 15, ALU.arith_shift_right)
        ts(w("wk", 0, H), wsum, 6, ALU.arith_shift_right, 511, ALU.bitwise_and)
        ts(w("wk", 2, H), wsum, 63, ALU.bitwise_and)
        for j in range(3):
            fill(V("wk" + h, W1 * j + H, W1 * j + W1), 0.0, "g")
        fill(V("wa" + h, W1 + H, 2 * W1), 0.0, "g")
        ts(V("kb" + h, 0, 10), ls(7), 32.0, ALU.add)

    def depth(hf):
        h = "_%d" % hf
        t0, t1 = V("tb" + h, 0, H), V("tb" + h, H, 2 * H)
        cp(t0, V("wk" + h, 2 * W1, 2 * W1 + H))
        scan(t1, t0, V("cv"), -1.0, ALU.max, ALU.add)
        e = V("tb" + h, H + 15, 2 * H, 16)
        fill(V("ck" + h), 0.0)
        tt(V("ck" + h, 0, 10), c3, e, ALU.subtract)
        lin(V("ck" + h, 16, 26), e, -1.0, -256.0)
        fill(V("sa" + h, 0, 30), -1.0e6)
        fill(V("sc" + h, 0, 30), -1.0e6)
        lin(V("sc" + h, 2, 30, 3), iw)

    def front(t, hf):
        h = "_%d" % hf
        now[0] = hf
        k = 2 * t + hf
        bank = 4 * hf
        X, Z, Z32 = V("x" + h), V("z" + h), V("z32" + h)
        quant(V("xq" + h), V("xs" + h), X)
        mm(bank, H, V("uq2"), V("us2"), V("xq" + h), V("xs" + h))
        for b in range(4):
            lin(V("xh" + h, 336 * b, 336 * b + H), (X[0], b, 640, 4), 0.5)
            if not SAME:
                dup(V("xi" + h, H * b, H * b + H), V("xh" + h, 336 * b, 336 * b + H), "cp%d" % (4 * hf + b) if XDMA else None)
        if t == 0:
            dma("y", [V("xq" + h, 0, 48)], [V("landq", 288 * hf, 288 * hf + 48)],
                lambda T: (T.landq[:, 288 * hf:288 * hf + 48].bitcast(dt.uint8), T["xq" + h][:, 0:48].bitcast(dt.uint8)), "ld%d" % (7 + 2 * hf), 2200.0)
            dma("y", [V("xs" + h, 0, 48)], [V("lands", 288 * hf, 288 * hf + 48)],
                lambda T: (T.lands[:, 288 * hf:288 * hf + 48], T["xs" + h][:, 0:48]), "ld%d" % (8 + 2 * hf), 2200.0)
        M = V("mx" + h)
        scan(M, V("ps", 512 * bank, 512 * bank + H), V("cm"), -1.0e29, ALU.max, ALU.add)
        top, cnt = C("sm" + h, 96), C("sm" + h, 100)
        op({"v": vc(5)}, [M], [top], lambda q, T, e: q.tensor_reduce(ap(T, top), ap(T, (M[0], 31, H, 32)), AxisListType.X, ALU.max))
        op({"s": par["act"] + 20 + H * cy}, [M, top], [V("junk" + h), cnt],
           lambda q, T, e: q.activation(ap(T, V("junk" + h)), ap(T, M), ACT.Sign, bias=ap(T, top), scale=-1.0, accum_out=ap(T, cnt)))
        lr = lambda a, b: V("lr" + h, a, b)
        ts(lr(0, 4), V("cf", 20, 24), cnt, ALU.add)
        ts(lr(4, 20), V("wa" + h), C("cf", 32 + ADMAS[hf]), ALU.mult, -1.0, ALU.add, idx=lr(0, 1))
        rank = V("ka" + h, 0, 10)
        if t == 0 and hf in MARK0:
            lin(V("mk" + h, 0, H), V("w0", 0, W1), idx=lr(4, 14))
            scan(V("mk" + h, H, 2 * H), V("keep"), V("mk" + h, 0, H), 0.0, ALU.mult, ALU.add)
            cp(V("si" + h, 0, 5), V("mk" + h, H + 31, 2 * H, 32))
            ts(V("si" + h, 16, 26, 2), V("si" + h, 0, 5), 6, ALU.arith_shift_right, 511, ALU.bitwise_and)
            ts(V("si" + h, 17, 26, 2), V("si" + h, 0, 5), 15, ALU.arith_shift_right)
            tt(rank, V("si" + h, 16, 26), V("kb" + h, 0, 10), ALU.max)
        else:
            tt(V("ka" + h, 0, 16), V("wk" + h, 0, 2 * W1), V("kb" + h, 0, 16), ALU.max, idx=lr(0, 1))
        ts(lr(20, 30), rank, 32.0, ALU.subtract)
        for b in range(4):
            lin(V("xh" + h, 336 * b + W1, 336 * b + 336), V("xh" + h, 336 * b, 336 * b + W1), idx=lr(4, 14))
            tt((Z[0], b, 640, 4), V("xh" + h, 336 * b, 336 * b + 336), V("xh" + h, 336 * b, 336 * b + H) if SAME else V("xi" + h, H * b, H * b + H), ALU.add, idx=lr(20, 30))
            lin((Z32[0], H * b, H * b + H, 1), (Z[0], b, 640, 4), 32.0)
        if t == 2:
            iota(V("pw" + h, 0, W1), [[1, W1]], H * hf)
            lin(V("pw" + h, W1, W1 + H), V("pw" + h, 0, W1), idx=lr(4, 14))
            lin(V("fob", H * hf, H * hf + H), V("pw" + h), idx=lr(20, 30))
        quant(V("zq" + h), V("zs" + h), Z)
        base = 4 * (288 * hf + 48 + 80 * t)
        for b in range(4):
            mm(bank + b, H, V("wq", 128 * b, 128 * b + 128), V("wsc", 128 * b, 128 * b + 128), V("zq" + h), V("zs" + h))
        for b in range(4):
            tt(V("win" + h, 256 * b, 256 * b + H), V("ps", 512 * (bank + b), 512 * (bank + b) + H), (Z32[0], H * b, H * b + H, 1), ALU.add)
            lin(V("pt", base + b, base + 320, 4), V("win" + h, 256 * b, 256 * b + W1), 1.0 / 32, idx=lr(14, 19))
        quant(V("pq", 128 * k, 128 * k + 128), V("psc", 128 * k, 128 * k + 128), V("pt", base - 192, base + 320))
        a, la = 128 * k + 48, 288 * hf + 48 + 80 * t
        op({"g": par["iss"]}, [V("pq", a, a + 80), V("psc", a, a + 80)], [V("landq", la, la + 80), V("lands", la, la + 80)], None,
           kind="rem", sem="arr%d" % k, lat=par["rem"] + (par["first"] if k == 0 else 0.0), step=STEP[t], moves=[("pq", a, "landq", la, 80), ("psc", a, "lands", la, 80)])
        lin(V("p16" + h), V("pt", base, base + 320), 16.0)
        if t == 0:
            depth(hf)
        tt(V("sa" + h, 2, 98, 3), V("wk" + h), V("ck" + h), ALU.add, idx=lr(2, 4))
        lin(V("sa" + h, 1, 30, 3), V("sa" + h, 50, 80, 3), -1024.0, 16384.0)
        lin(V("sc" + h, 0, 30, 3), rank, 1024.0, -1024.0 * (W1 + 31))
        scan(V("sm" + h, 128, 158), V("sa" + h, 0, 30), V("sc" + h, 0, 30), 0.0, ALU.min, ALU.max)
        cp(lr(70, 80), V("sm" + h, 130, 158, 3))

    def back(t, hf):
        h = "_%d" % hf
        now[0] = hf
        bank = 4 * hf
        la = 288 * hf + 48 + 80 * t
        for b in range(4):
            mm(bank + b, 128, V("eq", 128 * b, 128 * b + 128), V("es", 128 * b, 128 * b + 128), V("landq", la - 48, la + 80), V("lands", la - 48, la + 80))
        for b in range(4):
            tt(V("win" + h, 256 * b + W1, 256 * b + 256), V("ps", 512 * (bank + b) + 48, 512 * (bank + b) + 128), V("p16" + h, b, 320, 4), ALU.add)
            lin(V("x" + h, b, 640, 4), V("win" + h, 256 * b, 256 * b + 256), 1.0 / 32, idx=V("lr" + h, 70, 80))

    def finish(hf):
        h = "_%d" % hf
        now[0] = hf
        a = H * hf
        quant(V("xq" + h), V("xs" + h), V("x" + h))
        mm(4 * hf, H, V("vq"), V("vs"), V("xq" + h), V("xs" + h))
        dma("ys", [V("xq" + h)], [], lambda T: (T.oc[:, 4 * a:4 * a + 4 * H], T["xq" + h][:].bitcast(dt.uint8)), "out", 2200.0)
        for j in range(4):
            dma("ys", [V("xs" + h)], [], lambda T, j=j: (T.osc[4 * j:4 * j + 4, a:a + H], T["xs" + h][32 * j:32 * j + 4, :]), "out", 2000.0)
        lin(V("yb", a, a + H), V("ps", 2048 * hf, 2048 * hf + H))
        dma("ys", [V("yb", a, a + H)], [], lambda T: (T.y[:, a:a + H], T.yb[:, a:a + H]), "out", 2200.0)

    for hf in range(2):
        tree(hf)
    for t in range(3):
        for hf in range(2):
            if t:
                back(t - 1, hf)
            front(t, hf)
    dma("y", [V("fob")], [], lambda T: (T.fo[:], T.fob[0:128:16, :]), "out", 2000.0)
    for hf in range(2):
        back(2, hf)
        finish(hf)
    return ops


def depend(ops):
    writer = {n: np.full(s[1][1], -1) for n, s in SCRATCH.items()}
    readers = {n: [] for n in SCRATCH}
    for i, o in enumerate(ops):
        dep = set(o.get("after", []))
        rd = [a for a in o["rd"] if a[0] != "ps"]
        wr = [a if a[0] != "ps" else ("ps", a[1] // 512 * 512, a[1] // 512 * 512 + 512, 1) for a in o["wr"] + [a for a in o["rd"] if a[0] == "ps"]]
        for a in rd + wr:
            dep.update(int(j) for j in np.unique(writer[a[0]][a[1]:a[2]:a[3]]) if j >= 0)
        for a in wr:
            m = np.zeros(len(writer[a[0]]), bool)
            m[a[1]:a[2]:a[3]] = True
            dep.update(j for j, b in readers[a[0]] if m[b[1]:b[2]:b[3]].any())
        for a in rd:
            readers[a[0]].append((i, a))
        for a in wr:
            writer[a[0]][a[1]:a[2]:a[3]] = i
        dep.discard(i)
        o["dep"] = sorted(dep)


def place(ops, seq, par, pre, eng, bias, back=False, tail=False):
    hop = par["hop"]
    lo, hi = {e: [] for e in "vspgy"}, {e: [] for e in "vspgy"}
    n = len(ops)
    start, done, out = [0.0] * n, [0.0] * n, [None] * n
    for i in seq:
        ready = 0.0
        for j in pre[i]:
            if done[j] > ready:
                ready = done[j]
        if pre[i]:
            ready += hop
        dur, lat = ops[i]
        best = None
        for e in (dur if eng[i] is None else eng[i]):
            d = dur[e]
            st = ready + lat[e] if back else ready
            a, b = lo[e], hi[e]
            k = m = len(a)
            if tail and m:
                st = max(st, b[-1])
            while k > 0 and b[k - 1] > st:
                k -= 1
            while k < m and a[k] < st + d:
                if b[k] > st:
                    st = b[k]
                k += 1
            key = st + d * (bias if e == "v" else 1.0) + (0.0 if back else lat[e])
            if best is None or key < best[0]:
                best = (key, st, e, d, k)
        key, st, e, d, k = best
        lo[e].insert(k, st)
        hi[e].insert(k, st + d)
        start[i], done[i], out[i] = st, st + d + (0.0 if back else lat[e]), e
    return start, done, out


def replay(ops, order, eng, par, pre, chain=False):
    hop = par["hop"]
    free, last = dict.fromkeys("vspgy", 0.0), dict.fromkeys("vspgy", -1)
    n = len(ops)
    done, why = [0.0] * n, [-1] * n
    for i in order:
        e = eng[i]
        st, w = free[e] - hop, last[e]
        for j in pre[i]:
            if done[j] > st:
                st, w = done[j], j
        dur, lat = ops[i]
        free[e] = st + hop + dur[e]
        done[i], why[i], last[e] = free[e] + lat[e], w, i
    end = max(done)
    if not chain:
        return end
    i, pairs = done.index(end), []
    while why[i] >= 0:
        if why[i] not in pre[i]:
            pairs.append((why[i], i))
        i = why[i]
    return end, pairs


def arrange(ops, par, others, tries):
    n = len(ops)
    pre, anc = [], []
    for o in ops:
        a = 0
        for j in o["dep"]:
            a |= anc[j]
        pre.append([j for j in o["dep"] if not a >> j & 1])
        for j in o["dep"]:
            a |= 1 << j
        anc.append(a)
    succ = [[] for _ in ops]
    for i in range(n):
        for j in pre[i]:
            succ[j].append(i)
    half = [o["hf"] for o in ops]
    others = [([(o["dur"], o["lat"]) for o in q], p) for q, p in others]
    ops = others[0][0]
    tail = [0.0] * n
    for i in range(n - 1, -1, -1):
        tail[i] = min(ops[i][0][e] + ops[i][1][e] for e in ops[i][0]) + max([tail[j] + par["hop"] for j in succ[i]] + [0.0])
    x = [SEED]

    def rnd():
        x[0] = (x[0] * 1103515245 + 12345) % 2147483648
        return x[0] / 2147483648.0

    def legal(pr):
        pr = list(pr)
        for i in range(n - 1, -1, -1):
            for j in succ[i]:
                if pr[i] >= pr[j]:
                    pr[i] = pr[j] - 1e-3
        return [i for _, i in sorted(zip(pr, range(n)))]
    flex = [i for i in range(n) if len(ops[i][0]) > 1]
    best, top = None, None
    for it in range(tries):
        if it < 40:
            pr = [-tail[i] + 1000.0 * (it % 10) * half[i] for i in range(n)]
            bias, fix = 1.0 + 0.7 * (it // 10), [None] * n
        else:
            pr, fix, bias = list(best[3]), list(best[2]), 1.0
            a, w = rnd() * best[4], 300 + 3000 * rnd() * rnd()
            u = rnd()
            if u < MIX[0] and best[6]:
                i, j = best[6][int(rnd() * len(best[6]))]
                v = rnd()
                k = i if rnd() < 0.5 else j
                if v < 0.4 and len(ops[k][0]) > 1:
                    alt = [e for e in ops[k][0] if e != fix[k]]
                    fix[k] = alt[int(rnd() * len(alt))]
                elif v < 0.7:
                    pr[j] = pr[i] - 1.0 - 600.0 * rnd() * rnd()
                else:
                    pr[i] = pr[j] + 1.0 + 600.0 * rnd() * rnd()
            elif u < MIX[1]:
                amp = 100 + 1500 * rnd()
                pr = [s + (amp * (rnd() - 0.5) if a < s < a + w else 0.0) for s in pr]
            elif u < MIX[2]:
                amp, hf = 2000 * (rnd() - 0.5), int(rnd() * 2)
                pr = [s + (amp if a < s < a + w and half[i] == hf else 0.0) for i, s in enumerate(pr)]
            else:
                for _ in range(1 + int(rnd() * 2)):
                    i = flex[int(rnd() * len(flex))]
                    alt = [e for e in ops[i][0] if e != fix[i]]
                    fix[i] = alt[int(rnd() * len(alt))]
        start, done, eng = place(ops, legal(pr), par, pre, fix, bias)
        if it < 40 or it % JUST == 0:
            s2, d2, e2 = place(ops, legal([start[i] + ops[i][0][eng[i]] for i in range(n)])[::-1], par, succ, eng, 1.0, True)
            start, done, eng = place(ops, legal([-d for d in d2]), par, pre, eng, 1.0)
        order = [i for _, i in sorted(zip(start, range(n)))]
        cost = sum(replay(q, order, eng, p, pre) for q, p in others) / len(others)
        if best is None or cost <= best[0] + (0.0 if it < 40 else TEMP * (1.0 - it / tries) * rnd() * 2.0):
            q, p = others[it % len(others)]
            best = (cost, order, eng, start, max(done), done, replay(q, order, eng, p, pre, True)[1])
            if top is None or cost < top[0]:
                top = best
    cost, order, eng = top[0], list(top[1]), list(top[2])
    keep = (cost, order, eng)
    pairs = top[6]
    for at in range(MOVES * AGAIN):
        it = at % MOVES
        if at and not it:
            cost, order, eng = keep
            pairs = replay(ops, order, eng, par, pre, True)[1]
        if not pairs:
            break
        i, j = pairs[int(rnd() * len(pairs))]
        u = rnd()
        o2, e2 = order, eng
        if u < 0.25:
            k = i if rnd() < 0.5 else j
            if len(ops[k][0]) < 2:
                continue
            alt = [e for e in ops[k][0] if e != eng[k]]
            e2 = list(eng)
            e2[k] = alt[int(rnd() * len(alt))]
        else:
            a, b = order.index(i), order.index(j)
            far = int(12 * rnd() * rnd() * rnd())
            if u < 0.6:
                a = max(0, a - far)
                m = anc[j] | 1 << j
                mid = order[a:b + 1]
                o2 = order[:a] + [k for k in mid if m >> k & 1] + [k for k in mid if not m >> k & 1] + order[b + 1:]
            else:
                b = min(n - 1, b + far)
                mid = order[a:b + 1]
                o2 = order[:a] + [k for k in mid if k != i and not anc[k] >> i & 1] + [k for k in mid if k == i or anc[k] >> i & 1] + order[b + 1:]
        c = sum(replay(q, o2, e2, p, pre) for q, p in others) / len(others)
        if c <= cost + TEMP2 * (1.0 - it / MOVES) * rnd() * rnd():
            cost, order, eng = c, o2, e2
            q, p = others[it % len(others)]
            pairs = replay(q, order, eng, p, pre, True)[1]
            if cost < keep[0]:
                keep = (cost, order, eng)
    cost, order, eng = keep
    start, done, out = place(ops, order, par, pre, eng, 1.0, False, True)
    return order, eng, done, cost


def plan(tries):
    sets = []
    for ch in SETS:
        p = dict(PAR)
        p.update(ch)
        q = build(p)
        depend(q)
        sets.append((q, p))
    return (sets[0][0],) + arrange(sets[0][0], PAR, sets, tries)


OPS, ORDER, ENG, DONE, COST = plan(TRIES)


def rank_program(g, core, T, topo):
    rank = T.rank_of(core)
    if rank is None:
        return
    queue = {"v": g.vector, "s": g.scalar, "p": g.tensor, "g": g, "y": g.sync}
    count = dict.fromkeys(["v", "s", "p", "g", "out", "sent"], 0)
    mark, known = {}, {}
    seen = {e: {} for e in queue}
    for i in ORDER:
        o, e = OPS[i], ENG[i]
        q = queue[e]
        for j in sorted(o["dep"], key=lambda j: -DONE[j]):
            s, c = mark[j]
            if seen[e].get(s, 0) < c:
                q.wait_ge(T.sem[s], c)
                seen[e][s] = c
                for s2, c2 in known[j].items():
                    seen[e][s2] = max(seen[e].get(s2, 0), c2)
        known[i] = dict(seen[e])
        if o["kind"] == "c" and e != "y":
            o["emit"](q, T, e).then_inc(T.sem[e], 1)
            count[e] += 1
            mark[i] = (e, count[e])
        elif o["kind"] != "rem":
            o["emit"](q, T, e).then_inc(T.sem[o["sem"]], 16)
            count[o["sem"]] = count.get(o["sem"], 0) + 16
            mark[i] = (o["sem"], count[o["sem"]])
        else:
            peer = T.cores[rank ^ o["step"]]
            rid, pid = topo.addr(peer, core)
            m, n = topo.mask(core, peer), len(topo.engines(core, peer))
            a, la, w = o["moves"][0][1], o["moves"][0][3], o["moves"][0][4]
            g.remote_dma(T.landq[:, la:la + w].bitcast(dt.uint8), T.pq[:, a:a + w].bitcast(dt.uint8), T.sem[o["sem"]], T.sem.sent, pid, rid, m)
            g.remote_dma(T.lands[:, la:la + w], T.psc[:, a:a + w], T.sem[o["sem"]], T.sem.sent, pid, rid, m)
            count["sent"] += 2 * n
            mark[i] = (o["sem"], 2 * n)
            known[i] = {}
    for s in ("g", "sent", "v", "s", "p", "out"):
        g.wait_ge(T.sem[s], count[s])
